import numpy as np, ml_dtypes
CORES = [40,64,80,88,96,104,120,144]
N = 8
import mx_ref
BF = ml_dtypes.bfloat16
def gentries(a):
    return np.ascontiguousarray(a.reshape(8, 16, -1).transpose(0, 2, 1)).reshape(8, -1)
def gtable(e):
    e = np.asarray(e); return np.ascontiguousarray(e.reshape(8, -1, 16).transpose(0, 2, 1)).reshape(128, -1).astype(np.int32)
def gcols(t, e):
    v = np.concatenate([t.reshape(8, 16, -1, 4), np.zeros((8, 16, 1, 4), BF)], axis=2)
    return np.ascontiguousarray(np.stack([v[g][:, e[g]] for g in range(8)])).reshape(128, -1)
def tile(rs):
    return np.stack(rs, axis=2).reshape(128, -1).astype(BF)
def cut(t, i, w=512):
    return t[:, w * i:w * i + w]
def pick(q, e):
    c = np.concatenate([q[0].reshape(128, -1, 4), np.zeros((128, 1, 4), np.uint8)], axis=1); s = np.concatenate([q[1], np.ones((16, 1), np.uint8)], axis=1)
    return (np.ascontiguousarray(c[:, e].reshape(128, -1)), np.ascontiguousarray(s[:, e]))
def join(*qs):
    return (np.concatenate([q[0] for q in qs], axis=1), np.concatenate([q[1] for q in qs], axis=1))
def put(q, e, v):
    c, s = q[0].reshape(128, -1, 4).copy(), q[1].copy(); c[:, e] = v[0].reshape(128, -1, 4); s[:, e] = v[1]
    return (c.reshape(128, -1), s)
def pk(c, s):
    return (np.ascontiguousarray(c), mx_ref.live(s))
def emit(q):
    return q[0], q[1]
def packed(v, rng):
    q = [mx_ref.quantize(np.ascontiguousarray(v[r])) for r in range(N)]
    return np.stack([a for a, b in q]), np.stack([mx_ref.plane(b, rng) for a, b in q])
def values_of_codes():
    e, c = np.zeros((128, 128, 4), np.float32), np.zeros((128, 2, 4), np.uint8)
    e[np.arange(128), np.arange(128), 0] = 1
    c[:127, :, 0] = np.arange(256).reshape(2, 128).T[:127]
    return mx_ref.matmul(mx_ref.quantize(e.reshape(128, 512).astype(BF)), (c.reshape(128, 8), np.full((16, 2), 127, np.uint8))).T.reshape(-1).astype(np.float64)
CODE_VALUE, SCALE_VALUE = values_of_codes(), 2.0 ** (np.arange(256) - 127.0)
def decode(q):
    return (CODE_VALUE[q[0]].reshape(16, 8, -1, 4) * SCALE_VALUE[q[1]][:, None, :, None] + 0.0).reshape(128, -1).astype(np.float32)
def f(rng, *shape):
    return mx_ref.flush((rng.standard_normal(shape, dtype=np.float32) * np.exp2(rng.integers(-2, 3, shape[:-1] + (1,)))).astype(BF))
def wide(rng, *shape, cols=0):
    v = rng.standard_normal(shape, dtype=np.float32) * np.exp2(rng.integers(-12, 13, shape)).astype(np.float32)
    if cols: v *= np.repeat(np.exp2(rng.integers(-cols, cols + 1, shape[:-2] + (1, shape[-1] // 4))) * (rng.random(shape[:-2] + (1, shape[-1] // 4)) > 0.0625), 4, axis=-1).astype(np.float32)
    return mx_ref.flush(v.astype(BF))
C, A, R, T = 192, 64, 3, 6
STEP = [1, 2, 4]
def turn(p, s):
    at = np.argmax((s + np.float32(0.0)).reshape(8, T, 32), axis=2) + 32 * np.arange(T)
    back, on, new, way = at, np.ones((8, T), bool), p.copy(), np.full((8, T, 32), -1)
    for i in range(32):
        way[:, :, i] = np.where(on, at, -1)
        np.put_along_axis(new, at, back, axis=1)
        up = np.take_along_axis(p, at, axis=1)
        back = np.where(up == at, back, at)
        on = on & (up != at)
        at = up
    slot, home = np.full((8, A), -1), np.full((8, C), -1)
    for g in range(8):
        n = 0
        for k in range(T):
            w = way[g, k][way[g, k] >= 0][:A - n]
            slot[g, n:n + len(w)] = w
            home[g, w] = n + len(w) - 1 - np.arange(len(w))
            n += len(w)
    return new, slot, home
def numbers_of(rng):
    return {"x": np.array(f(rng, N, 128, 4 * C)), "u": np.array(f(rng, N, 128, 512)), "v": np.array(f(rng, N, 128, 512))}
def packing(rng, w):
    c, p = packed(w, rng)
    return {"wc": c, "ws": p}
def weights(rng, off=None, deaf=False):
    w = np.array(f(rng, N, 128, 2048)).reshape(N, 128, 4, 128, 4)
    if off is not None:
        w[:, :, :, off] = 0
        if deaf: w[:, off] = 0
    return packing(rng, w.reshape(N, 128, 2048))
def forest(rng):
    o = np.argsort(rng.random((N, 8, T, 32)), axis=3)
    i = np.arange(32)
    n = rng.choice([1, 2, 3, 32], (N, 8, T, 1))
    b = np.minimum(1 + rng.integers(0, n, o.shape), i)
    p = np.zeros_like(o)
    np.put_along_axis(p, o, np.take_along_axis(o, i - b, axis=3), axis=3)
    return p
def stored(p):
    return np.stack([gtable((p[r] + 32 * np.arange(T)[:, None]).reshape(8, C)) for r in range(N)])
def signs(rng):
    return np.stack([rng.permutation(8) % 2 * 2.0 - 1.0 for r in range(N)])
def setup_inputs(rng):
    return {**numbers_of(rng), "par": stored(forest(rng)), **weights(rng)}
def setup_inputs_ties(rng):
    d = numbers_of(rng)
    e = rng.permutation(N)
    x = d["x"].reshape(N, 8, 16, C, 4)
    for r in range(N):
        k = rng.permutation(C) % 3
        if e[r] == 0: k[:] = 0
        a = x[r][:, :8, :3].copy()
        a[:, :, 2] = 0
        if e[r] == 1: a[:] = 0
        x[r][:, :8] = a[:, :, k]
    u = d["u"].reshape(N, 8, 16, 128, 4)
    for t in range(R): u[:, :, 8:, t::16] = 0
    return {"x": x.reshape(N, 128, 4 * C), "u": u.reshape(N, 128, 512), "v": d["v"], "par": stored(forest(rng)), **weights(rng, np.arange(128) % 16 < 8)}
def setup_inputs_near(rng):
    d = numbers_of(rng)
    x = d["x"].astype(np.float32).reshape(N, 8, 16, C, 4)
    s = np.argsort(rng.random((N, 8, R, T, 32)), axis=4) // 2
    up = (np.arange(N)[:, None, None] + np.arange(8)[:, None] + np.arange(R)) % 2 == int(rng.integers(2))
    s = np.where(up[..., None, None], np.arange(32) // 2, s).reshape(N, 8, R, C)
    x[:, :, 0] = 0
    x[:, :, 0, :, 0] = signs(rng)[:, :, None]
    x[:, :, 8:8 + R] = ((s[..., None] >> np.arange(4)) & 1) * np.exp2(np.arange(4) - 23.0)
    x[:, :, 8 + R:] = rng.integers(4, 8, (N, 8, 8 - R, C, 4)) * rng.choice([-1.0, 1.0], (N, 8, 8 - R, C, 4)) * 2.0 ** -20
    for g in rng.permutation(8)[:4]:
        x[:, int(g), 0, 32 * np.arange(T) + rng.integers(0, 32, T), 0] = -2.0 ** 30
    k = np.where(rng.permutation(N) < N // 2, 2.0 ** -30, 1.0).astype(np.float32).astype(BF)
    u = d["u"].reshape(N, 128, 128, 4)
    for t in range(R):
        u[:, :, t::16] = 0
        for h in range(0, 128, 16):
            u[:, h, h + t, 0] = k
            u[:, h + 8 + t, h + t] = k[:, None]
    i = np.arange(128) % 16
    return {"x": x.reshape(N, 128, 4 * C).astype(BF), "u": u.reshape(N, 128, 512), "v": d["v"], "par": stored(forest(rng)), **weights(rng, (i == 0) | (i >= 8), True)}
def setup_inputs_shapes(rng):
    d, p = numbers_of(rng), forest(rng)
    e, q = rng.permutation(N), int(rng.integers(8))
    x = d["x"].reshape(N, 8, 16, C, 4)
    u = d["u"].reshape(N, 128, 128, 4)
    for t in range(R): u[:, :, t::16] = 0
    for r in range(N):
        kinds = rng.permutation(8)
        if e[r] == 0: kinds[:] = 4
        if e[r] == 1: kinds[:] = 3
        chain = np.argsort(rng.random((8, T, 32)), axis=2)
        for g in range(8):
            h, at = int(kinds[g]), np.zeros(T, int)
            if h < 7: np.put_along_axis(p[r, g], chain[g], chain[g][:, np.maximum(np.arange(32) - 1, 0)], axis=1)
            if h == 7: chain[g, :, 0] = np.argmax(p[r, g] == np.arange(32), axis=1)
            for t in range(R):
                if h < 3:
                    cutoff = rng.permutation(np.repeat(np.arange(T), 16))[:17 * T - (A, A + 1, A - 1)[h]]
                    n = 16 - np.bincount(cutoff, minlength=T)
                    at = np.where((at + n <= 31) & ((at < n) | (rng.random(T) < 0.5)), at + n, at - n)
                elif h in (4, 5):
                    at = 31 - at
                    if h == 5: at[0] = int(rng.integers(32))
                elif h > 5: at = rng.integers(0, 32, T)
                low = int(rng.integers(2))
                mark = -rng.integers(2, 4, C).astype(np.float32) if low else rng.integers(-1, 2, C).astype(np.float32)
                mark[32 * np.arange(T) + chain[g, np.arange(T), at]] = (2.0, -1.0)[low]
                k = R * g + t
                x[r, q, k // 4, :, k % 4] = mark.astype(BF)
                u[r, 16 * q + k // 4, 16 * g + t, k % 4] = 1.0
    return {"x": x.reshape(N, 128, 4 * C), "u": u.reshape(N, 128, 512), "v": d["v"], "par": stored(p), **weights(rng, np.arange(128) // 8 == 2 * q)}
def setup_inputs_huge(rng):
    d = numbers_of(rng)
    x = 2.0 ** 30 * (0.6 + 0.35 * rng.random((N, 128, C, 4)))
    mixed = rng.permutation(N) < N // 2
    side = (np.argsort(rng.random((N, T, 32)), axis=2) % 2).reshape(N, C)
    first = np.arange(128) % 16 < 8
    x *= (~mixed[:, None, None] | (first[None, :, None] == (side[:, None, :] == 1)))[..., None]
    u = d["u"].reshape(N, 128, 128, 4)
    for t in range(R):
        c = signs(rng)[:, None, :] * np.where(mixed[:, None, None] & ~first[None, :, None], -1.0, 1.0)
        u[:, :, t::16] = (2.0 ** 30 * (0.75 + 0.25 * rng.random((N, 128, 8, 4))) * c[..., None]).astype(np.float32).astype(BF)
    w = np.zeros((N, 128, 4, 128, 4), np.float32)
    i = np.arange(128)
    for b in range(4): w[:, i, b, i, b] = 0.125
    return {"x": x.astype(np.float32).reshape(N, 128, 4 * C).astype(BF), "u": u.reshape(N, 128, 512), "v": d["v"], "par": stored(forest(rng)), **packing(rng, w.reshape(N, 128, 2048).astype(BF))}
def setup_inputs_spread(rng):
    d = setup_inputs(rng)
    d["x"] = wide(rng, N, 128, 4 * C, cols=6)
    return d
def check_inputs(d):
    b = []
    for k in ("x", "u", "v"):
        a = np.abs(d[k].astype(np.float32))
        if not (np.isfinite(a).all() and ((a == 0) | (a >= 2.0 ** -30) & (a <= 2.0 ** 30)).all()): b.append("a value of " + k)
    if np.isin(d["wc"], [127, 255]).any(): b.append("wc: a code that is no number")
    for r in range(N):
        a = np.abs(decode(pk(d["wc"][r], d["ws"][r])))
        if not ((a == 0) | (a >= 2.0 ** -30) & (a <= 2.0 ** 30)).all(): b.append("wc and ws: a number out of range")
        p = gentries(d["par"][r]).astype(np.int64)
        if (p // 32 != np.arange(C) // 32).any():
            b.append("par: a parent outside the tree")
            continue
        a = p
        for i in range(5): a = np.take_along_axis(a, a, axis=1)
        z = a.reshape(8, T, 32)
        if (z != z[:, :, :1]).any() or (np.take_along_axis(p, a, axis=1) != a).any(): b.append("par: a tree without one root that all its nodes come to")
    return b
def reference(x, u, v, par, wc, ws):
    qu = [mx_ref.quantize(u[r]) for r in range(N)]
    lay = [pk(wc[r], ws[r]) for r in range(N)]
    now = [x[r] for r in range(N)]
    parent = [gentries(par[r]).astype(np.int64) for r in range(N)]
    for t in range(R):
        sent, homes, made = [], [], []
        for r in range(N):
            q = mx_ref.quantize(now[r])
            parent[r], slot, home = turn(parent[r], mx_ref.matmul(qu[r], q)[t::16])
            homes.append(home)
            sent.append(mx_ref.quantize(gcols(decode(q).astype(BF), slot)))
        for r in range(N):
            p = sent[r ^ STEP[t]]
            h = tile([np.maximum(mx_ref.matmul(pick(lay[r], np.arange(128 * b, 128 * b + 128)), p), np.float32(0.0)) * np.float32(0.03125) for b in range(4)])
            made.append(mx_ref.quantize(h))
        came = decode(join(*made)).astype(BF)
        for r in range(N):
            got = gcols(cut(came, r ^ STEP[t], 4 * A), homes[r])
            now[r] = (now[r].astype(np.float32) + got.astype(np.float32)).astype(BF)
    y, op = np.zeros((N, 128, C), np.float32), np.zeros((N, 8, C), np.float32)
    oc, osc = np.zeros((N, 128, 4 * C), np.uint8), np.zeros((N, 16, C), np.uint8)
    for r in range(N):
        q = mx_ref.quantize(now[r])
        y[r] = mx_ref.matmul(mx_ref.quantize(v[r]), q)
        op[r] = parent[r]
        oc[r], osc[r] = emit(q)
    return {"y": y, "op": op, "oc": oc, "osc": osc}

@@ -1,0 +1,517 @@
+from concourse.bass import DstId, RemoteDMATransfer
+from concourse.mybir import dt, AluOpType, ActivationFunctionType
+
+F32, BF, I32, U16, U8, FP8 = "float32", "bfloat16", "int32", "uint16", "uint8", "float8_e4m3fn_x4"
+C, A, R = 192, 64, 3
+STEP = [1, 2, 4]
+BIG = 9.0e29
+
+
+def sb(n, d):
+    return ("sbuf", [128, n], d)
+
+
+SCRATCH = {
+    "ps": ("psum", [128, 4096], F32),
+    "pari": sb(12, I32), "ub": sb(512, BF), "vb": sb(512, BF), "wq": sb(512, FP8), "wsc": sb(512, U8),
+    "xw0": sb(1024, BF), "xw1": sb(1024, BF), "xw2": sb(1024, BF), "xw3": sb(768, BF),
+    "uq": sb(128, FP8), "us": sb(128, U8), "vq": sb(128, FP8), "vs": sb(128, U8),
+    "upq": sb(384, FP8), "ups": sb(384, U8), "eq": sb(512, FP8), "es": sb(512, U8),
+    "lq": sb(C + 5 * A, FP8), "ls": sb(C + 5 * A, U8), "oq": sb(6 * 128, FP8), "osn": sb(6 * 128, U8),
+    "rq": sb(6 * A, FP8), "rs": sb(6 * 256, U8), "gq": sb(C, FP8), "gs": sb(C, U8), "gl": sb(16, U16),
+    "fq": sb(C, FP8), "fs": sb(C, U8), "fo": sb(16, U16),
+    "xq1": sb(C, FP8), "xs1": sb(C, U8), "xq2": sb(C, FP8), "xs2": sb(C, U8), "xq3": sb(C, FP8), "xs3": sb(C, U8),
+    "pi": sb(2, I32), "ci": sb(12, I32), "cf": sb(12, F32), "cf1": sb(12, F32), "cd": sb(12, F32),
+    "iot": sb(256, F32), "jm16": sb(C, BF), "jm4": sb(C, BF), "kap": sb(C, BF), "zt": sb(520, BF),
+    "ti": sb(128, F32), "tj": sb(128, F32), "oi": sb(36, I32), "oc16": sb(36, U16), "osm": sb(8, U16),
+    "h16": sb(C, BF), "h4": sb(C, BF), "ha": sb(C, BF), "hb": sb(C, BF), "cap": sb(C, F32), "ge": sb(C, BF), "m1": sb(C, BF),
+    "w1": sb(12, U16), "w2": sb(12, U16), "w4": sb(12, U16), "w8": sb(12, U16),
+    "p1": sb(384, BF), "p2": sb(C, BF), "p4": sb(C, BF), "p8": sb(C, BF), "sc": sb(C, BF),
+    "im": sb(C, BF), "inn": sb(C, BF), "ta": sb(C, BF), "tm": sb(C, BF), "tn": sb(C, BF), "t2a": sb(C, F32), "tw": sb(392, F32),
+    "eb": sb(C, F32), "npr": sb(C, BF), "cb": sb(C, BF), "boff": sb(2, U16), "pw": sb(16, U16), "pf": sb(272, BF),
+    "fl": sb(C, BF), "cum": sb(264, BF), "rootf": sb(C, BF), "vl": sb(34, F32), "rr": sb(34, F32), "es1": sb(32, F32),
+    "ew": sb(4, U16), "slf": sb(A, BF), "sls": sb(A, F32), "slo": sb(16, U16), "slo0": sb(16, U16),
+    "m_t": sb(32, F32), "m_n": sb(32, F32), "m_s": sb(32, F32), "mw": sb(4, U16), "mf": sb(A, BF), "ms4": sb(A, F32), "ms16": sb(A, BF),
+    "mo4": sb(16, U16), "mo16": sb(4, U16), "srf": sb(256, BF), "srs": sb(C, F32), "sro": sb(48, U16),
+    "q_t": sb(16, F32), "q_i": sb(16, F32), "q_d": sb(16, F32), "q_o": sb(16, F32), "qo": sb(12, U16), "vals": sb(C, BF),
+    "dx": sb(1024, BF), "ph": sb(768, BF), "xm": sb(256, BF), "yf": sb(C, F32), "opf": sb(C, F32),
+}
+LOADS = ["par", "x", "u", "wc", "ws", "v"]
+STORES = ["y", "op", "oc", "s0", "s1", "s2", "s3"]
+SEMAPHORES = (["cv", "cs", "ct", "cg", "lo", "ral", "lal"] + ["d_" + n for n in LOADS + STORES]
+              + ["ra%d" % s for s in range(6)] + ["la%d" % s for s in range(6)])
+
+
+def helpers(T, rank, topo):
+    core = T.cores[rank]
+    ok = [c for c in topo.cores_of(core) if c != core and all(topo.may_write(c, T.cores[rank ^ s]) for s in STEP)]
+    ok.sort(key=lambda c: (topo.die(c) != topo.die(core), c))
+    return ok[:2]
+
+
+def bits(engines):
+    return sum(1 << e for e in engines)
+
+
+def live(s):
+    return 0 if s % 2 == 0 else A
+
+
+def landing(s):
+    return C + A * (s - 1)
+
+
+def helper_program(g, core, T, topo, rank, which):
+    every = len(topo.engines(T.cores[rank], core))
+    sent = [0]
+
+    def hand(out, src, came, k, lands, dst):
+        rid, pid = topo.addr(dst, core)
+        g.wait_ge(T.sem[came], k)
+        g.remote_dma(out, src, T.sem[lands], T.sem.lo, pid, rid, topo.mask(core, dst))
+        sent[0] += len(topo.engines(core, dst))
+
+    dst = T.cores[rank ^ STEP[0]]
+    if which == 0:
+        hand(T.fq[:].bitcast(dt.uint8), T.gq[:].bitcast(dt.uint8), "ra0", every // 2, "la0", dst)
+        hand(T.fo[:], T.gl[:], "ral", every, "lal", dst)
+    else:
+        hand(T.fs[:], T.gs[:], "ra0", every // 2, "la0", dst)
+    for s in range(1, 6):
+        lo = landing(s)
+        if which == 0:
+            src, out = T.rq[:, A * s:A * s + A].bitcast(dt.uint8), T.lq[:, lo:lo + A].bitcast(dt.uint8)
+        else:
+            a = 256 * s + 128 + live(s)
+            src, out = T.rs[:, a:a + A], T.ls[:, lo:lo + A]
+        hand(out, src, "ra%d" % s, every // 2, "la%d" % s, T.cores[rank ^ STEP[s // 2]])
+    g.wait_ge(T.sem.lo, sent[0])
+
+
+def rank_program(g, core, T, topo):
+    rank = T.rank_of(core)
+    if rank is None:
+        for r in range(len(T.cores)):
+            hs = helpers(T, r, topo)
+            if core in hs:
+                helper_program(g, core, T, topo, r, hs.index(core))
+        return
+    hs = helpers(T, rank, topo)
+    Q = {"v": g.vector, "s": g.scalar, "t": g.tensor, "g": g, "y": g.sync}
+    CNT = {"v": "cv", "s": "cs", "t": "ct", "g": "cg"}
+    ops = []
+    touched = {}
+
+    def B(name, lo=0, hi=None, step=1):
+        if hi is None:
+            hi = SCRATCH[name][1][1]
+        ap = T[name][:, lo:hi] if step == 1 else T[name][:, lo:hi:step]
+        return (ap, [(name, lo, hi, step)])
+
+    def col(name, j):
+        return B(name, j, j + 1)
+
+    def ind(win, off):
+        return (win[0].indirect(off[0]), win[1], off[1])
+
+    def w32(v):
+        return (v[0].bitcast(dt.uint32), v[1])
+
+    def meet(a, b):
+        if a[1] <= b[0] or b[1] <= a[0]:
+            return False
+        return not (a[2] == b[2] and a[2] > 1 and (a[0] - b[0]) % a[2])
+
+    def note(me, regions, writes, deps):
+        for name, lo, hi, step in regions:
+            seen = touched.setdefault(name, [])
+            for e in seen:
+                if e[3] != me and (writes or e[4]) and meet((lo, hi, step), e):
+                    deps.append(e[3])
+            if writes:
+                seen[:] = [e for e in seen if not (step == 1 and lo <= e[0] and e[1] <= hi)]
+            seen.append((lo, hi, step, me, writes))
+
+    def add(q, call, outs, ins, sem=None):
+        me, deps = len(ops), []
+        for v in ins:
+            if isinstance(v, tuple):
+                note(me, v[1] + (v[2] if len(v) > 2 else []), False, deps)
+        for v in outs:
+            if len(v) > 2:
+                note(me, v[2], False, deps)
+            note(me, v[1], True, deps)
+        ops.append([q, call, deps, sem, False])
+
+    def arrival(name, t, k, *views):
+        add(None, None, list(views), [], (name, sum(len(topo.engines(h, core)) for h in helpers(T, rank ^ STEP[t], topo)[:k])))
+
+    def a_(v):
+        return v[0] if isinstance(v, tuple) else v
+
+    O = AluOpType
+    IDENT = ActivationFunctionType.Identity
+
+    def copy(out, in_):
+        add("v", lambda: g.vector.tensor_copy(out[0], in_[0]), [out], [in_])
+
+    def tt(out, x, y, op):
+        add("v", lambda: g.vector.tensor_tensor(out[0], x[0], y[0], op), [out], [x, y])
+
+    def ts(out, x, s1, op0, s2=None, op1=None):
+        if op1 is None:
+            add("v", lambda: g.vector.tensor_scalar(out[0], x[0], a_(s1), None, op0), [out], [x, s1])
+        else:
+            add("v", lambda: g.vector.tensor_scalar(out[0], x[0], a_(s1), a_(s2), op0, op1), [out], [x, s1, s2])
+
+    def scan(out, d0, d1, init, op0, op1):
+        add("v", lambda: g.vector.tensor_tensor_scan(out[0], d0[0], d1[0], init, op0, op1), [out], [d0, d1])
+
+    def fill(out, c):
+        add("v", lambda: g.vector.memset(out[0], c), [out], [])
+
+    def quant(q, s, x):
+        add("v", lambda: g.vector.quantize_mx(q[0], s[0], x[0]), [q, s], [x])
+
+    def lin(out, in_, scale, bias):
+        add("s", lambda: g.scalar.activation(out[0], in_[0], IDENT, bias=a_(bias), scale=a_(scale)), [out], [in_, scale, bias])
+
+    def act(out, in_, func=ActivationFunctionType.Copy, scale=None):
+        if scale is None:
+            add("s", lambda: g.scalar.activation(out[0], in_[0], func), [out], [in_])
+        else:
+            add("s", lambda: g.scalar.activation(out[0], in_[0], func, scale=a_(scale)), [out], [in_, scale])
+
+    def mm(bank, w, lq_, ls_, rq_, rs_):
+        out = B("ps", 512 * bank, 512 * bank + w)
+        add("t", lambda: g.tensor.matmul_mx(out[0], lq_[0], ls_[0], rq_[0], rs_[0], True, True),
+            [B("ps", 512 * bank, 512 * bank + 512)], [lq_, ls_, rq_, rs_])
+
+    def iota(out, pattern, base, cm, whole=False):
+        if whole:
+            add("g", lambda: g.iota(out[0], pattern, base, cm), [out], [])
+        else:
+            add("g", lambda: g.iota(out[0], pattern, base, cm, allow_small_or_imprecise_dtypes=True), [out], [])
+
+    def dma(q, name, out, in_, outs, ins):
+        add(q, lambda: Q[q].dma_start(out, in_), outs, ins, ("d_" + name, 16))
+
+    eng = topo.engines(core, hs[0])
+    half = len(eng) // 2
+    (r0, p0), (r1, p1) = topo.addr(hs[0], core), topo.addr(hs[1], core)
+
+    def write(out, src, view, sem, pid, rid, engines):
+        add("g", lambda: g.remote_dma(out, src, T.sem[sem], T.sem.lo, pid, rid, bits(engines)), [], [view], ("lo", len(engines)))
+
+    def send(s):
+        base = 128 * s
+        cq = B("oq", base + live(s), base + live(s) + A)
+        cs = B("osn", base - 128, base + 128)
+        sem = T.sem["ra%d" % s]
+        add("g", lambda: g.remote_dma_fused([
+            RemoteDMATransfer(dst_ids=[DstId(rid=r0, pnc=p0)], dma_engine_mask=bits(eng[:half]), remote_sem=sem,
+                              src=cq[0].bitcast(dt.uint8), dst=T.rq[:, A * s:A * s + A].bitcast(dt.uint8)),
+            RemoteDMATransfer(dst_ids=[DstId(rid=r1, pnc=p1)], dma_engine_mask=bits(eng[half:]), remote_sem=sem,
+                              src=cs[0], dst=T.rs[:, 256 * s:256 * s + 256]),
+        ], local_sem=T.sem.lo), [], [cq, cs], ("lo", 2 * half))
+
+    def wrap16(out, free, tmp, width):
+        scan(B(tmp, 0, width), B("h16", 0, width), free, 0.0, O.add, O.min)
+        ts(out, B(tmp, 15, width, 16), col("cd", 4), O.add)
+
+    def wrap4(out, free, tmp, width):
+        scan(B(tmp, 0, width), B("h4", 0, width), free, 0.0, O.add, O.max)
+        ts(out, B(tmp, 3, width, 4), 4.0, O.mult, col("cd", 6), O.add)
+
+    dma("y", "par", T.pari[:], T.par[:], [B("pari")], [])
+    dma("s", "x", T.xw0[:, 0:4 * C], T.x[:], [B("xw0", 0, 4 * C)], [])
+    dma("y", "u", T.ub[:], T.u[:], [B("ub")], [])
+    dma("y", "wc", T.wq[:].bitcast(dt.uint8), T.wc[:], [B("wq")], [B("xw0", 0, 4 * C), B("ub")])
+    dma("y", "ws", T.wsc[:], T.ws[:], [B("wsc")], [])
+    dma("y", "v", T.vb[:], T.v[:], [B("vb")], [])
+
+    iota(col("pi", 0), [[0, 1]], 0, 1, True)
+    iota(B("iot"), [[1, 256]], 0, 0)
+    iota(B("jm16"), [[0, 12], [1, 16]], 0, 0)
+    iota(B("oi", 0, 24), [[1, 3], [16, 8]], 0, 0, True)
+    iota(B("oi", 24, 36), [[32, 6], [0, 2]], 0, 0, True)
+    iota(B("kap"), [[1, 6], [0, 32]], 0, 0)
+    iota(B("ti", 0, 32), [[-16, 4], [-32, 8]], 224, 0)
+    iota(B("ti", 32, 64), [[16, 4], [0, 8]], 0, 0)
+    for j, (sh, m) in enumerate([(0, 15), (0, 1), (1, 1), (2, 1), (3, 1), (0, 3), (2, 3), (1, 7), (0, 7), (0, 7)]):
+        ts(col("ci", j), col("pi", 0), sh, O.logical_shift_right, m, O.bitwise_and)
+    act(B("ph", 256, 512), B("iot"), IDENT, 0.0)
+    copy(B("cf", 0, 10), B("ci", 0, 10))
+    fill(B("cap"), BIG)
+    lin(B("cd", 0, 4), B("cf", 1, 5), -1.0, 1.0)
+    ts(B("cf1", 0, 10), B("cf", 0, 10), 1.0, O.add)
+    ts(col("cd", 4), col("cf", 0), 15.0, O.is_lt, 256.0, O.mult)
+    act(B("im"), B("iot", 0, C), IDENT, col("cf", 1))
+    act(B("inn"), B("iot", 0, C), IDENT, col("cd", 0))
+    act(B("pf", 16 + C, 272), B("iot", C, 256))
+    lin(col("cd", 7), col("cf", 7), 32.0, -32.0)
+    lin(col("cd", 5), col("cf", 6), 2048.0, 1280.0)
+    lin(col("cd", 9), col("cf", 6), 1024.0, -3072.0)
+    lin(col("cd", 8), col("cf", 1), 192.0, col("cd", 7))
+    lin(col("cd", 6), col("cf", 5), 1.0, col("cd", 9))
+    ts(B("osm", 0, 2), B("cf", 8, 10), -32.0, O.mult, 224.0, O.add)
+    ts(B("ha"), B("jm16"), col("cf", 0), O.is_le, 1280.0, O.mult)
+    ts(B("hb"), B("jm16"), col("cf1", 0), O.is_le, -256.0, O.mult)
+    fill(B("cap", 0, C, 32), -BIG)
+    tt(B("h16"), B("ha"), B("hb"), O.add)
+
+    def tables_head():
+        act(B("p2"), ind(B("p1", 0, C), B("w1")))
+        tt(B("ta"), ind(B("im"), B("w1")), B("inn"), O.add)
+
+    def tables(between):
+        between[0]()
+        for lv, (pa, pb, w) in enumerate([("p2", "p4", "w2"), ("p4", "p8", "w4"), ("p8", None, "w8")]):
+            act(B("tm"), B("ta"), IDENT, col("cf", 2 + lv))
+            wrap16(B(w), B(pa), "sc", C)
+            act(B("tn"), B("ta"), IDENT, col("cd", 1 + lv))
+            if pb:
+                act(B(pb), ind(B(pa), B(w)))
+            tt(B("ta") if pb else B("tw", 0, C), ind(B("tm"), B(w)), B("tn"), O.add)
+            between[1 + lv]()
+        act(B("t2a"), ind(B("tw", 0, C), B("w8")))
+        act(B("tw", C, 2 * C), ind(B("t2a"), B("w8")))
+
+    def pick_u(t):
+        off = B("oc16", 8 * t, 8 * t + 8)
+        copy(w32(B("upq", 128 * t, 128 * t + 128)), ind(w32(B("uq")), off))
+        act(B("ups", 128 * t, 128 * t + 128), ind(B("us"), off))
+
+    def xcodes(t):
+        return (B("lq", 0, C), B("ls", 0, C)) if t == 0 else (B("xq%d" % t), B("xs%d" % t))
+
+    def scores(t):
+        mm(4, C, B("upq", 128 * t, 128 * t + 128), B("ups", 128 * t, 128 * t + 128), *xcodes(t))
+
+    def unpack(w, q, s):
+        for b in range(4):
+            mm(b, w, B("eq", 128 * b, 128 * b + 128), B("es", 128 * b, 128 * b + 128), q, s)
+
+    def best_a():
+        scan(B("eb", 1, C), B("ps", 2048, 2048 + C - 1), B("cap", 1, C), -BIG, O.max, O.min)
+
+    def best_b():
+        tt(B("npr"), B("ps", 2048, 2048 + C), B("eb"), O.is_le)
+        scan(B("cb"), B("npr"), B("ge"), 0.0, O.min, O.add)
+        ts(col("boff", 0), col("cb", C - 1), -64.0, O.mult, col("cd", 8), O.add)
+
+    def dcopy(b):
+        act(B("dx", b, 4 * C, 4), B("ps", 512 * b, 512 * b + C))
+
+    PF = B("pf", 16, 272)
+    OS = B("osm", 0, 2)
+
+    def make_p(t, off):
+        copy(B("ph", 0, 128), ind(B("dx"), B(off, 0, 8)))
+        act(B("ph", 128, 256), ind(B("dx"), B(off, 8, 16)))
+        quant(B("oq", 256 * t, 256 * t + 128), B("osn", 256 * t, 256 * t + 128), B("ph", 0, 512))
+
+    def slots(t):
+        copy(B("pw"), ind(B("tw"), col("boff", 0)))
+        path = ind(B("iot"), B("pw", 0, 12))
+        if t == 0:
+            copy(B("pf", 16, 16 + C // 2), ind(B("iot"), B("pw", 0, 6)))
+            act(B("pf", 16 + C // 2, 16 + C), ind(B("iot"), B("pw", 6, 12)))
+            tt(B("fl"), B("pf", 16, 16 + C), B("pf", 15, 15 + C), O.is_equal)
+            scan(B("cum", 1, C + 1), B("fl"), B("ph", 256, 256 + C), 0.0, O.add, O.add)
+        else:
+            for b in range(3):
+                dcopy(b)
+            act(B("pf", 16, 16 + C), path)
+            dcopy(3)
+            tt(B("fl"), path, B("rootf"), O.is_equal)
+            scan(B("cum", 1, C + 1), B("fl"), B("m1"), 0.0, O.add, O.add)
+        tt(B("vl", 1, 33), ind(B("cum"), OS), B("tj", 0, 32), O.is_ge)
+        tt(B("rr", 1, 33), ind(B("cum"), OS), B("tj", 32, 64), O.add)
+        scan(B("es1"), B("vl", 0, 32), B("rr", 1, 33), 0.0, O.mult, O.max)
+        copy(B("ew"), B("es1", 7, 32, 8))
+        copy(B("slf"), ind(PF, B("ew")))
+        if t == 0:
+            wrap4(B("slo0"), B("slf"), "sls", A)
+            write(T.gl[:], T.slo0[:], B("slo0"), "ral", p0, r0, eng)
+        else:
+            wrap4(B("slo"), B("slf"), "sls", A)
+            make_p(t, "slo")
+            send(2 * t)
+
+    def lists(t, between):
+        xw = "xw%d" % t
+        act(B("vals"), B("pf", 15, 15 + C))
+        act(B("srf"), B("iot"))
+        tt(B("m_t"), B("rr", 0, 32), B("ti", 64, 96), O.subtract)
+        tt(B("q_t"), ind(B("cum"), col("osm", 4)), B("tj", 96, 112), O.subtract)
+        fill(B(xw, 4 * C, 1024), 0.0)
+        tt(B("m_n"), B("m_t"), B("tj", 64, 96), O.max)
+        tt(B("q_i"), ind(B("cum"), col("osm", 2)), B("q_t"), O.is_le)
+        scan(B("m_s"), B("vl", 0, 32), B("m_n"), 0.0, O.mult, O.min)
+        tt(B("q_d"), B("q_i"), B("tj", 112, 128), O.mult)
+        ts(B("mw"), B("m_s", 7, 32, 8), -1.0, O.mult)
+        tt(B("q_o"), ind(B("tw"), col("boff", 0)), B("q_d"), O.max)
+        act(B("vals", 0, C, 32), B("pf", 16, 16 + C, 32))
+        between()
+        act(B("mf"), ind(PF, B("mw")))
+        copy(B("qo"), B("q_o", 0, 12))
+        copy(ind(B("p1"), B("qo")), B("vals"))
+        wrap16(B("mo16"), B("mf"), "ms16", A)
+        wrap4(B("mo4"), B("mf"), "ms4", A)
+        copy(ind(B("srf"), B("mo16")), B("iot", C, 256))
+        act(B("xm"), ind(B(xw), B("mo4")))
+        if t + 1 < R:
+            wrap16(B("w1"), B("p1", 0, C), "sc", C)
+        wrap4(B("sro"), B("srf", 0, C), "srs", C)
+
+    def layer(t):
+        s = 2 * t
+        if t == 0:
+            arrival("lal", 0, 1, B("fo"))
+            make_p(0, "fo")
+            pq, psc, at = B("oq", 0, 128), B("osn", 0, 128), 0
+        else:
+            lo = landing(s)
+            arrival("la%d" % s, t, 2, B("lq", lo, lo + A), B("ls", lo, lo + A))
+            pq, psc, at = B("lq", lo - A, lo + A), B("ls", lo - A, lo + A), A
+        for b in range(4):
+            mm(4 + b, 128, B("wq", 128 * b, 128 * b + 128), B("wsc", 128 * b, 128 * b + 128), pq, psc)
+        for b in range(4):
+            lo = 512 * (4 + b) + at
+            act(B("ph", 512 + b, 768, 4), B("ps", lo, lo + A), ActivationFunctionType.Relu, 0.03125)
+        base = 128 * (s + 1)
+        quant(B("oq", base, base + 128), B("osn", base, base + 128), B("ph", 256, 768))
+        send(s + 1)
+
+    def update(t):
+        lo = landing(2 * t + 1)
+        arrival("la%d" % (2 * t + 1), t, 2, B("lq", lo, lo + A), B("ls", lo, lo + A))
+        unpack(128, B("lq", lo - A, lo + A), B("ls", lo - A, lo + A))
+        xw, nx = "xw%d" % t, "xw%d" % (t + 1)
+        for b in range(4):
+            tt(B(xw, 4 * C + b, 1024, 4), B("ps", 512 * b + A, 512 * b + 128), B("xm", b, 256, 4), O.add)
+        copy(B(nx, 0, 2 * C), ind(B(xw), B("sro", 0, 24)))
+        act(B(nx, 2 * C, 4 * C), ind(B(xw), B("sro", 24, 48)))
+        xq, xs = xcodes(t + 1)
+        quant(xq, xs, B(nx, 0, 4 * C))
+
+    def nothing():
+        return None
+
+    def unit(lo):
+        out, zero = B("zt", lo, lo + 256), B("ph", 256, 512)
+        add("g", lambda: g.affine_select(out[0], zero[0], [[1, 256]], O.not_equal, 1.0, lo - 3, -4), [out], [zero])
+
+    def first0():
+        quant(B("lq", 0, C), B("ls", 0, C), B("xw0", 0, 4 * C))
+        quant(B("uq"), B("us"), B("ub"))
+        write(T.gq[:].bitcast(dt.uint8), T.lq[:, 0:C].bitcast(dt.uint8), B("lq", 0, C), "ra0", p0, r0, eng[:half])
+        write(T.gs[:], T.ls[:, 0:C], B("ls", 0, C), "ra0", p1, r1, eng[half:])
+        for name, lo, hi, v in [("tw", 384, 392, 0), ("pf", 0, 16, -1), ("vl", 0, 1, 0), ("rr", 0, 1, 0), ("zt", 512, 520, 0)]:
+            iota(B(name, lo, hi), [[0, hi - lo]], v, 0)
+        iota(B("jm4"), [[0, 48], [2048, 4]], 0, 0)
+        iota(B("cum"), [[0, 264]], 0, 0)
+        iota(B("ti", 64, 96), [[0, 4], [-64, 8]], 479, 0)
+        iota(B("ti", 96, 112), [[0, 8], [-16, 2]], 32, 0)
+        iota(B("ti", 112, 128), [[16, 16]], C, 0)
+        unit(0)
+        unit(256)
+        copy(B("oc16"), B("oi"))
+
+    def first1():
+        pick_u(0)
+        scores(0)
+
+    def first2():
+        ts(B("ge"), B("kap"), col("cf", 7), O.is_equal, 1.0 / 64, O.mult)
+        fill(col("eb", 0), -BIG)
+        best_a()
+
+    def first3():
+        ts(B("ge", 31, C, 32), B("kap", 31, C, 32), col("cf", 7), O.is_equal, -63.0 / 64, O.mult)
+        ts(B("tj", 0, 32), B("ti", 0, 32), col("cf", 0), O.subtract)
+        best_b()
+        ts(B("tj", 32, 64), B("ti", 32, 64), col("cf", 0), O.add)
+        ts(B("h4"), B("jm4"), col("cd", 5), O.subtract, 256.0, O.min)
+
+    def unpack_partner():
+        for b in range(4):
+            dcopy(b)
+
+    copy(B("w1"), B("pari"))
+    act(B("p1", 0, C), ind(B("iot"), B("w1")))
+    tables_head()
+    tables([first0, first1, first2, first3])
+    for t in range(R):
+        if t > 0:
+            scores(t)
+            unpack(C, *xcodes(t))
+            best_a()
+            best_b()
+        slots(t)
+        if t == 0:
+            act(B("dx", 4 * C, 1024), B("iot"), IDENT, 0.0)
+            for b in range(4):
+                quant(B("eq", 128 * b, 128 * b + 128), B("es", 128 * b, 128 * b + 128), B("zt", 3 - b, 515 - b))
+            arrival("la0", 0, 2, B("fq"), B("fs"))
+            unpack(C, B("fq"), B("fs"))
+            lin(B("tj", 64, 96), B("tj", 0, 32), -1.0, -63.0)
+            lin(B("tj", 112, 128), B("ti", 112, 128), 1.0, col("cf", 0))
+            ts(B("tj", 96, 112), B("ti", 96, 112), col("cf", 0), O.subtract)
+            ts(col("osm", 2), col("cf", 7), 32.0, O.mult)
+            ts(col("osm", 4), col("cf1", 7), 32.0, O.mult)
+        lists(t, unpack_partner if t == 0 else nothing)
+        if t == 1:
+            tables_head()
+            pick_u(2)
+        layer(t)
+        if t + 1 < R:
+            act(B("rootf"), ind(PF, B("oc16", 24, 36)))
+            if t == 0:
+                tables_head()
+                tables([lambda: fill(B("m1"), 0.0), lambda: fill(B("m1", 0, C, 32), -1.0), nothing, lambda: pick_u(1)])
+            else:
+                tables([nothing, nothing, nothing, nothing])
+        else:
+            act(B("opf"), B("p1", 0, C))
+            dma("y", "op", T.op[:], T.opf[0:128:16, :], [], [B("opf")])
+            quant(B("vq"), B("vs"), B("vb"))
+        update(t)
+
+    xq, xs = xcodes(R)
+    mm(4, C, B("vq"), B("vs"), xq, xs)
+    dma("y", "oc", T.oc[:], xq[0].bitcast(dt.uint8), [], [xq])
+    for k in range(4):
+        dma("s" if k % 2 else "y", "s%d" % k, T.osc[4 * k:4 * k + 4, :], T.xs3[32 * k:32 * k + 4, :], [], [xs])
+    copy(B("yf"), B("ps", 2048, 2048 + C))
+    dma("s", "y", T.y[:], T.yf[:], [], [B("yf")])
+
+    for o in ops:
+        for d in o[2]:
+            ops[d][4] = True
+    token, total, waited = [], {}, {}
+    for o in ops:
+        name, k = o[3] if o[3] else (CNT[o[0]], 1 if o[4] else 0)
+        total[name] = total.get(name, 0) + k
+        token.append((name, total[name]))
+    for q, call, deps, sem, needed in ops:
+        if q is None:
+            continue
+        want = {}
+        for d in deps:
+            name, v = token[d]
+            want[name] = max(want.get(name, 0), v)
+        for name in sorted(want):
+            if waited.get((q, name), 0) < want[name]:
+                Q[q].wait_ge(T.sem[name], want[name])
+                waited[(q, name)] = want[name]
+        ins = call()
+        if sem is None:
+            if needed:
+                ins.then_inc(T.sem[CNT[q]], 1)
+        elif sem[0] != "lo":
+            ins.then_inc(T.sem[sem[0]], sem[1])
+    for name in sorted(total):
+        if total[name] and max([waited.get((q, name), 0) for q in Q]) < total[name]:
+            g.wait_ge(T.sem[name], total[name])

@@ -3,8 +3,13 @@ from concourse.mybir import dt, AluOpType, ActivationFunctionType
 
 F32, BF, I32, U16, U8, FP8 = "float32", "bfloat16", "int32", "uint16", "uint8", "float8_e4m3fn_x4"
 C, A, R = 192, 64, 3
+W = C + A
 STEP = [1, 2, 4]
 BIG = 9.0e29
+CYCLE, FIXED, GATHER, SCATTER = 0.00104, 0.07, 1.56, 3.8
+WAKE, ISSUE, CROSSING, FIRST_CROSSING, ALLOW, SLACK = 0.15, 0.15, 2.5, 5.0, 0.05, 0.25
+LOAD = {"par": 1.2, "x": 1.7, "u": 1.9}
+ORDER = []
 
 
 def sb(n, d):
@@ -14,27 +19,27 @@ def sb(n, d):
 SCRATCH = {
     "ps": ("psum", [128, 4096], F32),
     "pari": sb(12, I32), "ub": sb(512, BF), "vb": sb(512, BF), "wq": sb(512, FP8), "wsc": sb(512, U8),
-    "xw0": sb(1024, BF), "xw1": sb(1024, BF), "xw2": sb(1024, BF), "xw3": sb(768, BF),
+    "xw0": sb(4 * C, BF), "xw1": sb(4 * C, BF), "xw2": sb(4 * C, BF), "xw3": sb(4 * C, BF), "xp": sb(4 * W, BF),
     "uq": sb(128, FP8), "us": sb(128, U8), "vq": sb(128, FP8), "vs": sb(128, U8),
     "upq": sb(384, FP8), "ups": sb(384, U8), "eq": sb(512, FP8), "es": sb(512, U8),
     "lq": sb(C + 5 * A, FP8), "ls": sb(C + 5 * A, U8), "oq": sb(6 * 128, FP8), "osn": sb(6 * 128, U8),
-    "rq": sb(6 * A, FP8), "rs": sb(6 * 256, U8), "gq": sb(C, FP8), "gs": sb(C, U8), "gl": sb(16, U16),
-    "fq": sb(C, FP8), "fs": sb(C, U8), "fo": sb(16, U16),
+    "rq": sb(6 * A, FP8), "rs": sb(6 * 256, U8), "gq": sb(C, FP8), "gs": sb(C, U8), "gl": sb(8, U16),
+    "fq": sb(C, FP8), "fs": sb(C, U8), "fo": sb(8, U16),
     "xq1": sb(C, FP8), "xs1": sb(C, U8), "xq2": sb(C, FP8), "xs2": sb(C, U8), "xq3": sb(C, FP8), "xs3": sb(C, U8),
-    "pi": sb(2, I32), "ci": sb(12, I32), "cf": sb(12, F32), "cf1": sb(12, F32), "cd": sb(12, F32),
-    "iot": sb(256, F32), "jm16": sb(C, BF), "jm4": sb(C, BF), "kap": sb(C, BF), "zt": sb(520, BF),
-    "ti": sb(128, F32), "tj": sb(128, F32), "oi": sb(36, I32), "oc16": sb(36, U16), "osm": sb(8, U16),
-    "h16": sb(C, BF), "h4": sb(C, BF), "ha": sb(C, BF), "hb": sb(C, BF), "cap": sb(C, F32), "ge": sb(C, BF), "m1": sb(C, BF),
+    "pi": sb(2, I32), "ci": sb(8, I32), "cf": sb(8, F32), "cf1": sb(8, F32), "cd": sb(12, F32),
+    "iot": sb(W + C, BF), "jm16": sb(C, BF), "kap": sb(C, BF), "zt": sb(520, BF),
+    "ti": sb(128, F32), "tj": sb(128, F32), "oc16": sb(36, U16), "osm": sb(8, U16),
+    "h16": sb(C, BF), "ha": sb(C, BF), "hb": sb(C, BF), "cap": sb(C, F32), "ge0": sb(C, BF), "ge": sb(C, BF), "m1": sb(C, BF),
     "w1": sb(12, U16), "w2": sb(12, U16), "w4": sb(12, U16), "w8": sb(12, U16),
     "p1": sb(384, BF), "p2": sb(C, BF), "p4": sb(C, BF), "p8": sb(C, BF), "sc": sb(C, BF),
     "im": sb(C, BF), "inn": sb(C, BF), "ta": sb(C, BF), "tm": sb(C, BF), "tn": sb(C, BF), "t2a": sb(C, F32), "tw": sb(392, F32),
-    "eb": sb(C, F32), "npr": sb(C, BF), "cb": sb(C, BF), "boff": sb(2, U16), "pw": sb(16, U16), "pf": sb(272, BF),
+    "eb": sb(C, F32), "npr": sb(C, BF), "cb": sb(C, BF), "boff": sb(2, U16), "pw": sb(32, U16), "pf": sb(272, BF),
     "fl": sb(C, BF), "cum": sb(264, BF), "rootf": sb(C, BF), "vl": sb(34, F32), "rr": sb(34, F32), "es1": sb(32, F32),
-    "ew": sb(4, U16), "slf": sb(A, BF), "sls": sb(A, F32), "slo": sb(16, U16), "slo0": sb(16, U16),
-    "m_t": sb(32, F32), "m_n": sb(32, F32), "m_s": sb(32, F32), "mw": sb(4, U16), "mf": sb(A, BF), "ms4": sb(A, F32), "ms16": sb(A, BF),
-    "mo4": sb(16, U16), "mo16": sb(4, U16), "srf": sb(256, BF), "srs": sb(C, F32), "sro": sb(48, U16),
-    "q_t": sb(16, F32), "q_i": sb(16, F32), "q_d": sb(16, F32), "q_o": sb(16, F32), "qo": sb(12, U16), "vals": sb(C, BF),
-    "dx": sb(1024, BF), "ph": sb(768, BF), "xm": sb(256, BF), "yf": sb(C, F32), "opf": sb(C, F32),
+    "ew": sb(4, U16), "slf": sb(A, BF), "sls": sb(A, BF), "slo": sb(8, U16), "pws": sb(C, BF), "pwr": sb(16, F32),
+    "m_t": sb(32, F32), "m_n": sb(32, F32), "m_s": sb(32, F32), "mw": sb(4, U16), "mf": sb(A, BF), "ms": sb(A, BF),
+    "mo": sb(4, U16), "srf": sb(W, BF), "srs": sb(C, BF), "sro": sb(12, U16),
+    "q_t": sb(16, F32), "q_i": sb(16, F32), "q_d": sb(16, F32), "q_o": sb(16, F32), "qo": sb(12, U16),
+    "dx": sb(4 * C, BF), "dp": sb(4 * W, BF), "ph": sb(768, BF), "xm": sb(4 * A, BF), "yf": sb(C, F32), "opf": sb(C, F32),
 }
 LOADS = ["par", "x", "u", "wc", "ws", "v"]
 STORES = ["y", "op", "oc", "s0", "s1", "s2", "s3"]
@@ -74,9 +79,9 @@ def helper_program(g, core, T, topo, rank, which):
     dst = T.cores[rank ^ STEP[0]]
     if which == 0:
         hand(T.fq[:].bitcast(dt.uint8), T.gq[:].bitcast(dt.uint8), "ra0", every // 2, "la0", dst)
-        hand(T.fo[:], T.gl[:], "ral", every, "lal", dst)
     else:
         hand(T.fs[:], T.gs[:], "ra0", every // 2, "la0", dst)
+        hand(T.fo[:], T.gl[:], "ral", every, "lal", dst)
     for s in range(1, 6):
         lo = landing(s)
         if which == 0:
@@ -86,6 +91,51 @@ def helper_program(g, core, T, topo, rank, which):
             src, out = T.rs[:, a:a + A], T.ls[:, lo:lo + A]
         hand(out, src, "ra%d" % s, every // 2, "la%d" % s, T.cores[rank ^ STEP[s // 2]])
     g.wait_ge(T.sem.lo, sent[0])
+
+
+def plan(calls):
+    n = len(calls)
+    back = [[] for c in calls]
+    for i, c in enumerate(calls):
+        for d in c[3]:
+            back[n - 1 - d].append(n - 1 - i)
+    end = one_pass(calls, None)[1]
+    end = one_pass([calls[n - 1 - i][:3] + (back[i],) for i in range(n)], end[::-1])[1]
+    return one_pass(calls, end[::-1])[0]
+
+
+def one_pass(calls, given):
+    n = len(calls)
+    behind = [[] for c in calls]
+    for i, c in enumerate(calls):
+        for d in c[3]:
+            behind[d].append(i)
+    way = [0.0] * n
+    for i in reversed(range(n)):
+        way[i] = calls[i][1] + max([WAKE + way[j] for j in behind[i]], default=0.0)
+    way = given or way
+    end, free, order, todo = {}, {}, [], list(range(n))
+    while todo:
+        soonest = {}
+        for k in todo:
+            ready = max([(end[d] if d in end else soonest[d] + calls[d][1]) + WAKE for d in calls[k][3]], default=0.0)
+            soonest[k] = max(ready, free.get(calls[k][0], 0.0))
+        top = max(soonest[k] + way[k] for k in todo)
+        latest = {k: soonest[k] + ALLOW + SLACK * (top - soonest[k] - way[k]) for k in todo}
+        can = sorted((k for k in todo if all(d in end for d in calls[k][3])), key=lambda k: (soonest[k], -way[k]))
+
+        def done(i):
+            return soonest[i] + (calls[i][1] if calls[i][2] else ISSUE)
+
+        fits = [i for i in can if calls[i][0] is None
+                or not any(calls[k][0] == calls[i][0] and way[k] > way[i] and latest[k] < done(i) for k in todo)]
+        i = fits[0] if fits else max(can, key=lambda k: way[k])
+        end[i] = soonest[i] + calls[i][1]
+        if calls[i][0] is not None:
+            free[calls[i][0]] = done(i)
+        order.append(i)
+        todo.remove(i)
+    return order, [end[i] for i in range(n)]
 
 
 def rank_program(g, core, T, topo):
@@ -100,6 +150,7 @@ def rank_program(g, core, T, topo):
     Q = {"v": g.vector, "s": g.scalar, "t": g.tensor, "g": g, "y": g.sync}
     CNT = {"v": "cv", "s": "cs", "t": "ct", "g": "cg"}
     ops = []
+    left = {}
     touched = {}
 
     def B(name, lo=0, hi=None, step=1):
@@ -110,6 +161,9 @@ def rank_program(g, core, T, topo):
 
     def col(name, j):
         return B(name, j, j + 1)
+
+    def plane(name, b, width=W, lo=0, hi=None):
+        return B(name, width * b + lo, width * b + (width if hi is None else hi))
 
     def ind(win, off):
         return (win[0].indirect(off[0]), win[1], off[1])
@@ -132,7 +186,27 @@ def rank_program(g, core, T, topo):
                 seen[:] = [e for e in seen if not (step == 1 and lo <= e[0] and e[1] <= hi)]
             seen.append((lo, hi, step, me, writes))
 
-    def add(q, call, outs, ins, sem=None):
+    def width(v):
+        name, lo, hi, step = (v[2] if len(v) > 2 else v[1])[0]
+        return 16 * (hi - lo) if len(v) > 2 else -((lo - hi) // step)
+
+    def cost(q, outs, ins):
+        views = [v for v in ins if isinstance(v, tuple)]
+        wide = [v for v in views if width(v) > 1]
+        n = width(outs[0])
+        if len(outs[0]) > 2:
+            return FIXED + SCATTER * CYCLE * n
+        if any(len(v) > 2 for v in views):
+            return FIXED + GATHER * CYCLE * n
+        if q == "g":
+            return 2 * FIXED + 2 * CYCLE * n
+        if q == "t":
+            return CYCLE * (width(views[2]) + 16)
+        if q == "v" and len(wide) < 2 and all(SCRATCH[v[1][0][0]][2] in (BF, U16) for v in wide + outs):
+            n = n // 2
+        return max(FIXED, CYCLE * n)
+
+    def add(q, call, outs, ins, sem=None, time=None, after=()):
         me, deps = len(ops), []
         for v in ins:
             if isinstance(v, tuple):
@@ -141,10 +215,11 @@ def rank_program(g, core, T, topo):
             if len(v) > 2:
                 note(me, v[2], False, deps)
             note(me, v[1], True, deps)
-        ops.append([q, call, deps, sem, False])
+        ops.append([q, call, deps, sem, False, cost(q, outs, ins) if time is None else time, list(after)])
 
-    def arrival(name, t, k, *views):
-        add(None, None, list(views), [], (name, sum(len(topo.engines(h, core)) for h in helpers(T, rank ^ STEP[t], topo)[:k])))
+    def arrival(name, t, which, *views):
+        far = helpers(T, rank ^ STEP[t], topo)
+        add(None, None, list(views), [], (name, sum(len(topo.engines(far[k], core)) for k in which)), *left["r" + name[1:]])
 
     def a_(v):
         return v[0] if isinstance(v, tuple) else v
@@ -182,6 +257,15 @@ def rank_program(g, core, T, topo):
         else:
             add("s", lambda: g.scalar.activation(out[0], in_[0], func, scale=a_(scale)), [out], [in_, scale])
 
+    def move(q, out, in_):
+        (copy if q == "v" else act)(out, in_)
+
+    def times(q, out, in_, c):
+        if q == "v":
+            ts(out, in_, c, O.mult)
+        else:
+            act(out, in_, IDENT, c)
+
     def mm(bank, w, lq_, ls_, rq_, rs_):
         out = B("ps", 512 * bank, 512 * bank + w)
         add("t", lambda: g.tensor.matmul_mx(out[0], lq_[0], ls_[0], rq_[0], rs_[0], True, True),
@@ -194,14 +278,16 @@ def rank_program(g, core, T, topo):
             add("g", lambda: g.iota(out[0], pattern, base, cm, allow_small_or_imprecise_dtypes=True), [out], [])
 
     def dma(q, name, out, in_, outs, ins):
-        add(q, lambda: Q[q].dma_start(out, in_), outs, ins, ("d_" + name, 16))
+        add(q, lambda: Q[q].dma_start(out, in_), outs, ins, ("d_" + name, 16), LOAD.get(name, 1.2))
 
     eng = topo.engines(core, hs[0])
     half = len(eng) // 2
     (r0, p0), (r1, p1) = topo.addr(hs[0], core), topo.addr(hs[1], core)
 
     def write(out, src, view, sem, pid, rid, engines):
-        add("g", lambda: g.remote_dma(out, src, T.sem[sem], T.sem.lo, pid, rid, bits(engines)), [], [view], ("lo", len(engines)))
+        add("g", lambda: g.remote_dma(out, src, T.sem[sem], T.sem.lo, pid, rid, bits(engines)), [], [view],
+            ("lo", len(engines)), ISSUE)
+        left.setdefault(sem, (FIRST_CROSSING if sem == "ra0" else CROSSING, []))[1].append(len(ops) - 1)
 
     def send(s):
         base = 128 * s
@@ -213,167 +299,101 @@ def rank_program(g, core, T, topo):
                               src=cq[0].bitcast(dt.uint8), dst=T.rq[:, A * s:A * s + A].bitcast(dt.uint8)),
             RemoteDMATransfer(dst_ids=[DstId(rid=r1, pnc=p1)], dma_engine_mask=bits(eng[half:]), remote_sem=sem,
                               src=cs[0], dst=T.rs[:, 256 * s:256 * s + 256]),
-        ], local_sem=T.sem.lo), [], [cq, cs], ("lo", 2 * half))
+        ], local_sem=T.sem.lo), [], [cq, cs], ("lo", 2 * half), ISSUE)
+        left["ra%d" % s] = (CROSSING, [len(ops) - 1])
 
-    def wrap16(out, free, tmp, width):
-        scan(B(tmp, 0, width), B("h16", 0, width), free, 0.0, O.add, O.min)
-        ts(out, B(tmp, 15, width, 16), col("cd", 4), O.add)
+    def hold(tmp, free, n):
+        scan(B(tmp, 0, n), B("h16", 0, n), free, 0.0, O.add, O.min)
 
-    def wrap4(out, free, tmp, width):
-        scan(B(tmp, 0, width), B("h4", 0, width), free, 0.0, O.add, O.max)
-        ts(out, B(tmp, 3, width, 4), 4.0, O.mult, col("cd", 6), O.add)
+    def wrap(out, free, tmp, n):
+        hold(tmp, free, n)
+        ts(out, B(tmp, 15, n, 16), col("cd", 4), O.add)
 
-    dma("y", "par", T.pari[:], T.par[:], [B("pari")], [])
-    dma("s", "x", T.xw0[:, 0:4 * C], T.x[:], [B("xw0", 0, 4 * C)], [])
-    dma("y", "u", T.ub[:], T.u[:], [B("ub")], [])
-    dma("y", "wc", T.wq[:].bitcast(dt.uint8), T.wc[:], [B("wq")], [B("xw0", 0, 4 * C), B("ub")])
-    dma("y", "ws", T.wsc[:], T.ws[:], [B("wsc")], [])
-    dma("y", "v", T.vb[:], T.v[:], [B("vb")], [])
-
-    iota(col("pi", 0), [[0, 1]], 0, 1, True)
-    iota(B("iot"), [[1, 256]], 0, 0)
-    iota(B("jm16"), [[0, 12], [1, 16]], 0, 0)
-    iota(B("oi", 0, 24), [[1, 3], [16, 8]], 0, 0, True)
-    iota(B("oi", 24, 36), [[32, 6], [0, 2]], 0, 0, True)
-    iota(B("kap"), [[1, 6], [0, 32]], 0, 0)
-    iota(B("ti", 0, 32), [[-16, 4], [-32, 8]], 224, 0)
-    iota(B("ti", 32, 64), [[16, 4], [0, 8]], 0, 0)
-    for j, (sh, m) in enumerate([(0, 15), (0, 1), (1, 1), (2, 1), (3, 1), (0, 3), (2, 3), (1, 7), (0, 7), (0, 7)]):
-        ts(col("ci", j), col("pi", 0), sh, O.logical_shift_right, m, O.bitwise_and)
-    act(B("ph", 256, 512), B("iot"), IDENT, 0.0)
-    copy(B("cf", 0, 10), B("ci", 0, 10))
-    fill(B("cap"), BIG)
-    lin(B("cd", 0, 4), B("cf", 1, 5), -1.0, 1.0)
-    ts(B("cf1", 0, 10), B("cf", 0, 10), 1.0, O.add)
-    ts(col("cd", 4), col("cf", 0), 15.0, O.is_lt, 256.0, O.mult)
-    act(B("im"), B("iot", 0, C), IDENT, col("cf", 1))
-    act(B("inn"), B("iot", 0, C), IDENT, col("cd", 0))
-    act(B("pf", 16 + C, 272), B("iot", C, 256))
-    lin(col("cd", 7), col("cf", 7), 32.0, -32.0)
-    lin(col("cd", 5), col("cf", 6), 2048.0, 1280.0)
-    lin(col("cd", 9), col("cf", 6), 1024.0, -3072.0)
-    lin(col("cd", 8), col("cf", 1), 192.0, col("cd", 7))
-    lin(col("cd", 6), col("cf", 5), 1.0, col("cd", 9))
-    ts(B("osm", 0, 2), B("cf", 8, 10), -32.0, O.mult, 224.0, O.add)
-    ts(B("ha"), B("jm16"), col("cf", 0), O.is_le, 1280.0, O.mult)
-    ts(B("hb"), B("jm16"), col("cf1", 0), O.is_le, -256.0, O.mult)
-    fill(B("cap", 0, C, 32), -BIG)
-    tt(B("h16"), B("ha"), B("hb"), O.add)
-
-    def tables_head():
-        act(B("p2"), ind(B("p1", 0, C), B("w1")))
-        tt(B("ta"), ind(B("im"), B("w1")), B("inn"), O.add)
-
-    def tables(between):
-        between[0]()
-        for lv, (pa, pb, w) in enumerate([("p2", "p4", "w2"), ("p4", "p8", "w4"), ("p8", None, "w8")]):
-            act(B("tm"), B("ta"), IDENT, col("cf", 2 + lv))
-            wrap16(B(w), B(pa), "sc", C)
-            act(B("tn"), B("ta"), IDENT, col("cd", 1 + lv))
-            if pb:
-                act(B(pb), ind(B(pa), B(w)))
-            tt(B("ta") if pb else B("tw", 0, C), ind(B("tm"), B(w)), B("tn"), O.add)
-            between[1 + lv]()
-        act(B("t2a"), ind(B("tw", 0, C), B("w8")))
-        act(B("tw", C, 2 * C), ind(B("t2a"), B("w8")))
-
-    def pick_u(t):
-        off = B("oc16", 8 * t, 8 * t + 8)
-        copy(w32(B("upq", 128 * t, 128 * t + 128)), ind(w32(B("uq")), off))
-        act(B("ups", 128 * t, 128 * t + 128), ind(B("us"), off))
+    IDS = B("iot", 0, C)
+    PF = B("pf", 16, 272)
+    OS = B("osm", 0, 2)
+    PW = B("pw", 0, 12)
+    BEST = col("boff", 0)
 
     def xcodes(t):
         return (B("lq", 0, C), B("ls", 0, C)) if t == 0 else (B("xq%d" % t), B("xs%d" % t))
-
-    def scores(t):
-        mm(4, C, B("upq", 128 * t, 128 * t + 128), B("ups", 128 * t, 128 * t + 128), *xcodes(t))
 
     def unpack(w, q, s):
         for b in range(4):
             mm(b, w, B("eq", 128 * b, 128 * b + 128), B("es", 128 * b, 128 * b + 128), q, s)
 
-    def best_a():
-        scan(B("eb", 1, C), B("ps", 2048, 2048 + C - 1), B("cap", 1, C), -BIG, O.max, O.min)
-
-    def best_b():
-        tt(B("npr"), B("ps", 2048, 2048 + C), B("eb"), O.is_le)
-        scan(B("cb"), B("npr"), B("ge"), 0.0, O.min, O.add)
-        ts(col("boff", 0), col("cb", C - 1), -64.0, O.mult, col("cd", 8), O.add)
-
-    def dcopy(b):
-        act(B("dx", b, 4 * C, 4), B("ps", 512 * b, 512 * b + C))
-
-    PF = B("pf", 16, 272)
-    OS = B("osm", 0, 2)
-
-    def make_p(t, off):
-        copy(B("ph", 0, 128), ind(B("dx"), B(off, 0, 8)))
-        act(B("ph", 128, 256), ind(B("dx"), B(off, 8, 16)))
-        quant(B("oq", 256 * t, 256 * t + 128), B("osn", 256 * t, 256 * t + 128), B("ph", 0, 512))
-
-    def slots(t):
-        copy(B("pw"), ind(B("tw"), col("boff", 0)))
-        path = ind(B("iot"), B("pw", 0, 12))
-        if t == 0:
-            copy(B("pf", 16, 16 + C // 2), ind(B("iot"), B("pw", 0, 6)))
-            act(B("pf", 16 + C // 2, 16 + C), ind(B("iot"), B("pw", 6, 12)))
-            tt(B("fl"), B("pf", 16, 16 + C), B("pf", 15, 15 + C), O.is_equal)
-            scan(B("cum", 1, C + 1), B("fl"), B("ph", 256, 256 + C), 0.0, O.add, O.add)
+    def tables(first):
+        levels = [("p1", "w1"), ("p2", "w2"), ("p4", "w4"), ("p8", "w8")]
+        for lv, (p, w) in enumerate(levels):
+            if lv > 0 or not first:
+                wrap(B(w), B(p, 0, C), "sc", C)
+            if lv < 3:
+                act(B(levels[lv + 1][0]), ind(B(p, 0, C), B(w)))
+            if lv > 0:
+                times("s", B("tm"), B("ta"), col("cf", 1 + lv))
+                times("v", B("tn"), B("ta"), col("cd", lv))
+            m, n = ("tm", "tn") if lv else ("im", "inn")
+            tt(B("ta") if lv < 3 else B("tw", 0, C), ind(B(m), B(w)), B(n), O.add)
+        if first:
+            act(B("iot", W, W + C), ind(B("p8"), B("w8")))
         else:
-            for b in range(3):
-                dcopy(b)
-            act(B("pf", 16, 16 + C), path)
-            dcopy(3)
-            tt(B("fl"), path, B("rootf"), O.is_equal)
-            scan(B("cum", 1, C + 1), B("fl"), B("m1"), 0.0, O.add, O.add)
+            act(B("t2a"), ind(B("tw", 0, C), B("w8")))
+            act(B("tw", C, 2 * C), ind(B("t2a"), B("w8")))
+
+    def best(t):
+        mm(4, C, B("upq", 128 * t, 128 * t + 128), B("ups", 128 * t, 128 * t + 128), *xcodes(t))
+        scan(B("eb", 1, C), B("ps", 2048, 2048 + C - 1), B("cap", 1, C), -BIG, O.max, O.min)
+        tt(B("npr"), B("ps", 2048, 2048 + C), B("eb"), O.is_le)
+        scan(B("cb"), B("npr"), B("ge" if t else "ge0"), 0.0, O.min, O.add)
+        ts(BEST, col("cb", C - 1), -64.0, O.mult, col("cd", 8 if t else 5), O.add)
+
+    def places():
         tt(B("vl", 1, 33), ind(B("cum"), OS), B("tj", 0, 32), O.is_ge)
         tt(B("rr", 1, 33), ind(B("cum"), OS), B("tj", 32, 64), O.add)
         scan(B("es1"), B("vl", 0, 32), B("rr", 1, 33), 0.0, O.mult, O.max)
         copy(B("ew"), B("es1", 7, 32, 8))
-        copy(B("slf"), ind(PF, B("ew")))
-        if t == 0:
-            wrap4(B("slo0"), B("slf"), "sls", A)
-            write(T.gl[:], T.slo0[:], B("slo0"), "ral", p0, r0, eng)
-        else:
-            wrap4(B("slo"), B("slf"), "sls", A)
-            make_p(t, "slo")
-            send(2 * t)
 
-    def lists(t, between):
-        xw = "xw%d" % t
-        act(B("vals"), B("pf", 15, 15 + C))
-        act(B("srf"), B("iot"))
-        tt(B("m_t"), B("rr", 0, 32), B("ti", 64, 96), O.subtract)
+    def new_parents(t):
         tt(B("q_t"), ind(B("cum"), col("osm", 4)), B("tj", 96, 112), O.subtract)
-        fill(B(xw, 4 * C, 1024), 0.0)
-        tt(B("m_n"), B("m_t"), B("tj", 64, 96), O.max)
         tt(B("q_i"), ind(B("cum"), col("osm", 2)), B("q_t"), O.is_le)
-        scan(B("m_s"), B("vl", 0, 32), B("m_n"), 0.0, O.mult, O.min)
         tt(B("q_d"), B("q_i"), B("tj", 112, 128), O.mult)
-        ts(B("mw"), B("m_s", 7, 32, 8), -1.0, O.mult)
-        tt(B("q_o"), ind(B("tw"), col("boff", 0)), B("q_d"), O.max)
-        act(B("vals", 0, C, 32), B("pf", 16, 16 + C, 32))
-        between()
-        act(B("mf"), ind(PF, B("mw")))
+        if t == 0:
+            act(B("rootf", 0, C, 32), B("pf", 47, 47 + C, 32))
+            wrap(B("pwr", 0, 12), B("pf", 16, 16 + C), "pws", C)
+            tt(B("q_o", 0, 12), B("pwr", 0, 12), B("q_d", 0, 12), O.max)
+        else:
+            tt(B("q_o"), ind(B("tw"), BEST), B("q_d"), O.max)
         copy(B("qo"), B("q_o", 0, 12))
-        copy(ind(B("p1"), B("qo")), B("vals"))
-        wrap16(B("mo16"), B("mf"), "ms16", A)
-        wrap4(B("mo4"), B("mf"), "ms4", A)
-        copy(ind(B("srf"), B("mo16")), B("iot", C, 256))
-        act(B("xm"), ind(B(xw), B("mo4")))
-        if t + 1 < R:
-            wrap16(B("w1"), B("p1", 0, C), "sc", C)
-        wrap4(B("sro"), B("srf", 0, C), "srs", C)
+        copy(B("pf", 15, 15 + C, 32), B("pf", 16, 16 + C, 32))
+        copy(ind(B("p1"), B("qo")), B("pf", 15, 15 + C))
+        copy(B("pf", 47, 47 + C, 32), B("rootf", 0, C, 32))
+
+    def mirror(t):
+        tt(B("m_t"), B("rr", 0, 32), B("ti", 64, 96), O.subtract)
+        tt(B("m_n"), B("m_t"), B("tj", 64, 96), O.max)
+        scan(B("m_s"), B("vl", 0, 32), B("m_n"), 0.0, O.mult, O.min)
+        ts(B("mw"), B("m_s", 7, 32, 8), -1.0, O.mult)
+        copy(B("mf"), ind(PF, B("mw")))
+        wrap(B("mo"), B("mf"), "ms", A)
+        act(B("srf"), B("iot", 0, W))
+        copy(ind(B("srf"), B("mo")), B("iot", C, W))
+        wrap(B("sro"), B("srf", 0, C), "srs", C)
+        for b in range(4):
+            copy(plane("xp", b, hi=C), B("xw%d" % t, b, 4 * C, 4))
+            act(plane("xm", b, A), ind(plane("xp", b), B("mo")))
+
+    def make_p(t, off, queues):
+        for b, q in enumerate(queues):
+            move(q, B("ph", b, 4 * A, 4), ind(plane("dp", b), B(off, 0, 4)))
+        quant(B("oq", 256 * t, 256 * t + 128), B("osn", 256 * t, 256 * t + 128), B("ph", 0, 512))
 
     def layer(t):
         s = 2 * t
         if t == 0:
-            arrival("lal", 0, 1, B("fo"))
-            make_p(0, "fo")
             pq, psc, at = B("oq", 0, 128), B("osn", 0, 128), 0
         else:
             lo = landing(s)
-            arrival("la%d" % s, t, 2, B("lq", lo, lo + A), B("ls", lo, lo + A))
+            arrival("la%d" % s, t, [0, 1], B("lq", lo, lo + A), B("ls", lo, lo + A))
             pq, psc, at = B("lq", lo - A, lo + A), B("ls", lo - A, lo + A), A
         for b in range(4):
             mm(4 + b, 128, B("wq", 128 * b, 128 * b + 128), B("wsc", 128 * b, 128 * b + 128), pq, psc)
@@ -386,98 +406,137 @@ def rank_program(g, core, T, topo):
 
     def update(t):
         lo = landing(2 * t + 1)
-        arrival("la%d" % (2 * t + 1), t, 2, B("lq", lo, lo + A), B("ls", lo, lo + A))
+        arrival("la%d" % (2 * t + 1), t, [0, 1], B("lq", lo, lo + A), B("ls", lo, lo + A))
         unpack(128, B("lq", lo - A, lo + A), B("ls", lo - A, lo + A))
-        xw, nx = "xw%d" % t, "xw%d" % (t + 1)
+        nx = "xw%d" % (t + 1)
         for b in range(4):
-            tt(B(xw, 4 * C + b, 1024, 4), B("ps", 512 * b + A, 512 * b + 128), B("xm", b, 256, 4), O.add)
-        copy(B(nx, 0, 2 * C), ind(B(xw), B("sro", 0, 24)))
-        act(B(nx, 2 * C, 4 * C), ind(B(xw), B("sro", 24, 48)))
+            tt(plane("xp", b, lo=C), B("ps", 512 * b + A, 512 * b + 128), plane("xm", b, A), O.add)
+        for q, b, c0, c1 in [("s", 0, 0, 12), ("s", 1, 0, 12), ("v", 2, 0, 12), ("v", 3, 0, 8), ("s", 3, 8, 12)]:
+            move(q, B(nx, 64 * c0 + b, 64 * c1, 4), ind(plane("xp", b), B("sro", c0, c1)))
         xq, xs = xcodes(t + 1)
-        quant(xq, xs, B(nx, 0, 4 * C))
+        quant(xq, xs, B(nx))
 
-    def nothing():
-        return None
-
-    def unit(lo):
-        out, zero = B("zt", lo, lo + 256), B("ph", 256, 512)
-        add("g", lambda: g.affine_select(out[0], zero[0], [[1, 256]], O.not_equal, 1.0, lo - 3, -4), [out], [zero])
-
-    def first0():
-        quant(B("lq", 0, C), B("ls", 0, C), B("xw0", 0, 4 * C))
-        quant(B("uq"), B("us"), B("ub"))
-        write(T.gq[:].bitcast(dt.uint8), T.lq[:, 0:C].bitcast(dt.uint8), B("lq", 0, C), "ra0", p0, r0, eng[:half])
-        write(T.gs[:], T.ls[:, 0:C], B("ls", 0, C), "ra0", p1, r1, eng[half:])
-        for name, lo, hi, v in [("tw", 384, 392, 0), ("pf", 0, 16, -1), ("vl", 0, 1, 0), ("rr", 0, 1, 0), ("zt", 512, 520, 0)]:
-            iota(B(name, lo, hi), [[0, hi - lo]], v, 0)
-        iota(B("jm4"), [[0, 48], [2048, 4]], 0, 0)
-        iota(B("cum"), [[0, 264]], 0, 0)
-        iota(B("ti", 64, 96), [[0, 4], [-64, 8]], 479, 0)
-        iota(B("ti", 96, 112), [[0, 8], [-16, 2]], 32, 0)
-        iota(B("ti", 112, 128), [[16, 16]], C, 0)
-        unit(0)
-        unit(256)
-        copy(B("oc16"), B("oi"))
-
-    def first1():
-        pick_u(0)
-        scores(0)
-
-    def first2():
-        ts(B("ge"), B("kap"), col("cf", 7), O.is_equal, 1.0 / 64, O.mult)
-        fill(col("eb", 0), -BIG)
-        best_a()
-
-    def first3():
-        ts(B("ge", 31, C, 32), B("kap", 31, C, 32), col("cf", 7), O.is_equal, -63.0 / 64, O.mult)
-        ts(B("tj", 0, 32), B("ti", 0, 32), col("cf", 0), O.subtract)
-        best_b()
-        ts(B("tj", 32, 64), B("ti", 32, 64), col("cf", 0), O.add)
-        ts(B("h4"), B("jm4"), col("cd", 5), O.subtract, 256.0, O.min)
-
-    def unpack_partner():
-        for b in range(4):
-            dcopy(b)
-
-    copy(B("w1"), B("pari"))
-    act(B("p1", 0, C), ind(B("iot"), B("w1")))
-    tables_head()
-    tables([first0, first1, first2, first3])
-    for t in range(R):
-        if t > 0:
-            scores(t)
-            unpack(C, *xcodes(t))
-            best_a()
-            best_b()
-        slots(t)
-        if t == 0:
-            act(B("dx", 4 * C, 1024), B("iot"), IDENT, 0.0)
-            for b in range(4):
-                quant(B("eq", 128 * b, 128 * b + 128), B("es", 128 * b, 128 * b + 128), B("zt", 3 - b, 515 - b))
-            arrival("la0", 0, 2, B("fq"), B("fs"))
-            unpack(C, B("fq"), B("fs"))
-            lin(B("tj", 64, 96), B("tj", 0, 32), -1.0, -63.0)
-            lin(B("tj", 112, 128), B("ti", 112, 128), 1.0, col("cf", 0))
-            ts(B("tj", 96, 112), B("ti", 96, 112), col("cf", 0), O.subtract)
-            ts(col("osm", 2), col("cf", 7), 32.0, O.mult)
-            ts(col("osm", 4), col("cf1", 7), 32.0, O.mult)
-        lists(t, unpack_partner if t == 0 else nothing)
-        if t == 1:
-            tables_head()
-            pick_u(2)
+    def rest(t):
         layer(t)
+        new_parents(t)
+        mirror(t)
         if t + 1 < R:
             act(B("rootf"), ind(PF, B("oc16", 24, 36)))
-            if t == 0:
-                tables_head()
-                tables([lambda: fill(B("m1"), 0.0), lambda: fill(B("m1", 0, C, 32), -1.0), nothing, lambda: pick_u(1)])
-            else:
-                tables([nothing, nothing, nothing, nothing])
+            tables(False)
         else:
             act(B("opf"), B("p1", 0, C))
             dma("y", "op", T.op[:], T.opf[0:128:16, :], [], [B("opf")])
-            quant(B("vq"), B("vs"), B("vb"))
         update(t)
+
+    dma("y", "par", T.pari[:], T.par[:], [B("pari")], [])
+    dma("s", "x", T.xw0[:], T.x[:], [B("xw0")], [])
+    dma("y", "u", T.ub[:], T.u[:], [B("ub")], [])
+    dma("y", "wc", T.wq[:].bitcast(dt.uint8), T.wc[:], [B("wq")], [B("xw0"), B("ub")])
+    dma("y", "ws", T.wsc[:], T.ws[:], [B("wsc")], [B("xw0"), B("ub")])
+    dma("y", "v", T.vb[:], T.v[:], [B("vb")], [B("wq")])
+
+    iota(col("pi", 0), [[0, 1]], 0, 1, True)
+    iota(B("iot", 0, W), [[1, W]], 0, 0)
+    iota(B("jm16"), [[0, 12], [1, 16]], 0, 0)
+    iota(B("kap"), [[1, 6], [0, 32]], 0, 0)
+    iota(B("ti", 0, 32), [[-16, 4], [-32, 8]], 224, 0)
+    iota(B("ti", 32, 64), [[16, 4], [0, 8]], 0, 0)
+    iota(B("ti", 64, 96), [[0, 4], [-64, 8]], 479, 0)
+    iota(B("ti", 96, 112), [[0, 8], [-16, 2]], 32, 0)
+    iota(B("ti", 112, 128), [[16, 16]], C, 0)
+    iota(B("zt", 512, 520), [[0, 8]], 0, 0)
+    iota(B("tw", 384, 392), [[0, 8]], 0, 0)
+    for b in range(4):
+        iota(plane("dp", b, lo=C), [[0, A]], 0, 0)
+        iota(plane("xp", b, lo=C), [[0, A]], 0, 0)
+    for view, c in [(B("ph", 256, 512), 0.0), (B("cap"), BIG), (B("cap", 0, C, 32), -BIG), (B("cum"), 0.0), (col("eb", 0), -BIG),
+                    (B("pf", 0, 16), -1.0), (col("vl", 0), 0.0), (col("rr", 0), 0.0), (B("slo", 4, 8), 0),
+                    (B("m1"), 0.0), (B("m1", 0, C, 32), -1.0)]:
+        fill(view, c)
+    for j, (sh, m) in enumerate([(0, 15), (0, 1), (1, 1), (2, 1), (3, 1), (1, 7), (0, 7), (0, 7)]):
+        ts(col("ci", j), col("pi", 0), sh, O.logical_shift_right, m, O.bitwise_and)
+    copy(B("cf"), B("ci"))
+    lin(B("cd", 0, 4), B("cf", 1, 5), -1.0, 1.0)
+    lin(B("cf1"), B("cf"), 1.0, 1.0)
+    ts(col("cd", 4), col("cf", 0), 15.0, O.is_lt, 256.0, O.mult)
+    ts(col("cd", 6), col("cf", 6), 6.0, O.min)
+    lin(col("cd", 5), col("cd", 6), 32.0, -32.0)
+    lin(col("cd", 7), col("cf", 5), 32.0, -32.0)
+    lin(col("cd", 8), col("cf", 1), float(C), col("cd", 7))
+    times("v", B("im"), IDS, col("cf", 1))
+    times("v", B("inn"), IDS, col("cd", 0))
+    ts(B("ha"), B("jm16"), col("cf", 0), O.is_le, 1280.0, O.mult)
+    ts(B("hb"), B("jm16"), col("cf1", 0), O.is_le, -256.0, O.mult)
+    tt(B("h16"), B("ha"), B("hb"), O.add)
+    for name, j in [("ge0", 6), ("ge", 5)]:
+        ts(B(name), B("kap"), col("cf", j), O.is_equal, 1.0 / 64, O.mult)
+        ts(B(name, 31, C, 32), B("kap", 31, C, 32), col("cf", j), O.is_equal, -63.0 / 64, O.mult)
+    ts(B("osm", 0, 2), B("cf", 6, 8), -32.0, O.mult, 224.0, O.add)
+    ts(col("osm", 2), col("cf", 5), 32.0, O.mult)
+    ts(col("osm", 4), col("cf1", 5), 32.0, O.mult)
+    ts(B("tj", 0, 32), B("ti", 0, 32), col("cf", 0), O.subtract)
+    lin(B("tj", 32, 64), B("ti", 32, 64), 1.0, col("cf", 0))
+    lin(B("tj", 64, 96), B("tj", 0, 32), -1.0, -63.0)
+    ts(B("tj", 96, 112), B("ti", 96, 112), col("cf", 0), O.subtract)
+    lin(B("tj", 112, 128), B("ti", 112, 128), 1.0, col("cf", 0))
+    act(B("pf", 16 + C, 272), B("iot", C, W))
+    for t in range(R):
+        ts(B("oc16", 8 * t, 8 * t + 8), B("iot", 0, 128, 16), float(t), O.add)
+    for h in (0, 1):
+        ts(B("oc16", 24 + h, 36, 2), B("iot", 0, C, 32), 0.0, O.add)
+    for lo in (0, 256):
+        out, zero = B("zt", lo, lo + 256), B("ph", 256, 512)
+        add("g", lambda out=out, zero=zero, lo=lo: g.affine_select(out[0], zero[0], [[1, 256]], O.not_equal, 1.0, lo - 3, -4),
+            [out], [zero])
+    for b in range(4):
+        quant(B("eq", 128 * b, 128 * b + 128), B("es", 128 * b, 128 * b + 128), B("zt", 3 - b, 515 - b))
+    quant(B("uq"), B("us"), B("ub"))
+    quant(B("vq"), B("vs"), B("vb"))
+    for t in range(R):
+        off = B("oc16", 8 * t, 8 * t + 8)
+        copy(w32(B("upq", 128 * t, 128 * t + 128)), ind(w32(B("uq")), off))
+        act(B("ups", 128 * t, 128 * t + 128), ind(B("us"), off))
+
+    quant(B("lq", 0, C), B("ls", 0, C), B("xw0"))
+    write(T.gq[:].bitcast(dt.uint8), T.lq[:, 0:C].bitcast(dt.uint8), B("lq", 0, C), "ra0", p0, r0, eng[:half])
+    write(T.gs[:], T.ls[:, 0:C], B("ls", 0, C), "ra0", p1, r1, eng[half:])
+    copy(B("w1"), B("pari"))
+    act(B("p1", 0, C), ind(IDS, B("w1")))
+    tables(True)
+    best(0)
+    copy(B("pw", 0, 32, 2), ind(B("tw", 0, C), BEST))
+    ts(B("pw", 1, 32, 2), ind(B("tw", 0, C), BEST), float(W), O.add)
+    copy(B("pf", 16, 16 + C // 2), ind(B("iot"), B("pw", 0, 6)))
+    act(B("pf", 16 + C // 2, 16 + C), ind(B("iot"), B("pw", 6, 12)))
+    tt(B("fl"), B("pf", 16, 16 + C), B("pf", 15, 15 + C), O.is_equal)
+    scan(B("cum", 1, C + 1), B("fl"), B("ph", 256, 256 + C), 0.0, O.add, O.add)
+    places()
+    copy(B("slf"), ind(PF, B("ew")))
+    wrap(B("slo", 0, 4), B("slf"), "sls", A)
+    write(T.gl[:], T.slo[:], B("slo"), "ral", p1, r1, eng)
+    arrival("la0", 0, [0, 1], B("fq"), B("fs"))
+    unpack(C, B("fq"), B("fs"))
+    for b in range(4):
+        act(plane("dp", b, hi=C), B("ps", 512 * b, 512 * b + C))
+    arrival("lal", 0, [1], B("fo"))
+    make_p(0, "fo", "vsvs")
+    rest(0)
+
+    for t in range(1, R):
+        best(t)
+        unpack(C, *xcodes(t))
+        copy(B("pw", 0, 16), ind(B("tw"), BEST))
+        for b in range(4):
+            act(plane("dx", b, C), B("ps", 512 * b, 512 * b + C))
+        for b in range(4):
+            act(plane("dp", b, hi=C), ind(plane("dx", b, C), PW))
+        tt(B("fl"), ind(IDS, PW), B("rootf"), O.is_equal)
+        scan(B("cum", 1, C + 1), B("fl"), B("m1"), 0.0, O.add, O.add)
+        places()
+        make_p(t, "ew", "vvvs")
+        send(2 * t)
+        act(B("pf", 16, 16 + C), ind(IDS, PW))
+        rest(t)
 
     xq, xs = xcodes(R)
     mm(4, C, B("vq"), B("vs"), xq, xs)
@@ -487,15 +546,19 @@ def rank_program(g, core, T, topo):
     copy(B("yf"), B("ps", 2048, 2048 + C))
     dma("s", "y", T.y[:], T.yf[:], [], [B("yf")])
 
+    if not ORDER:
+        ORDER.extend(plan([(o[0], o[5], o[3] is None, sorted(set(o[2] + o[6]))) for o in ops]))
     for o in ops:
         for d in o[2]:
             ops[d][4] = True
-    token, total, waited = [], {}, {}
-    for o in ops:
+    token, total, waited = {}, {}, {}
+    for i in ORDER:
+        o = ops[i]
         name, k = o[3] if o[3] else (CNT[o[0]], 1 if o[4] else 0)
         total[name] = total.get(name, 0) + k
-        token.append((name, total[name]))
-    for q, call, deps, sem, needed in ops:
+        token[i] = (name, total[name])
+    for i in ORDER:
+        q, call, deps, sem, needed = ops[i][:5]
         if q is None:
             continue
         want = {}

@@ -1,4 +1,3 @@
-from concourse.bass import DstId, RemoteDMATransfer
 from concourse.mybir import dt, AluOpType, ActivationFunctionType
 
 F32, BF, I32, U16, U8, FP8 = "float32", "bfloat16", "int32", "uint16", "uint8", "float8_e4m3fn_x4"
@@ -6,10 +5,28 @@ C, A, R = 192, 64, 3
 W = C + A
 STEP = [1, 2, 4]
 BIG = 9.0e29
-CYCLE, FIXED, GATHER, SCATTER = 0.00104, 0.07, 1.56, 3.8
-WAKE, ISSUE, CROSSING, FIRST_CROSSING, ALLOW, SLACK = 0.15, 0.15, 2.5, 5.0, 0.05, 0.25
-LOAD = {"par": 1.2, "x": 1.7, "u": 1.9}
-ORDER = []
+
+FIRST = {
+    "v": "half iot ci cf w1 oc0 im ha hb inn cd4 h16 qx step0 hold1 qu tn1 take1 pick0 step1 ge0 oc1 hold2 eb take2 tn2 gend0 "
+         "npr step2 hold3 cb tn3 take3 boff step3 pick1 pw eq0 pf osm fl holdp cum takep pwr places qt eq1 es qi mt ew qd eq3 mn "
+         "qn eq2 qo ms scatter dp hold0' p take0' mw qp step0' mf hold1' split take1' tn1' qh holdm step1' takem hold2' isroot "
+         "take2' tn2' srf step2' hold3' holds tn3' take3' takes step3'",
+    "s": "zero cap q1 cd03 p1 negq double0 eb0 q8 capend sent tj112 tm1 picks0 double1 tm2 q2 cd5 double2 tm3 p16 pf cum0 tj32 "
+         "tj0 tj96 cd8 vals srf0 own tj64 picks1 dx dp p double0' relu tm1' double1' m1 tm2' double2' tm3' xm",
+    "g": "pi jm16 ti0 tail ti64 kap sendx unit1 tw0 unit0 small xpz sendp sende dpz sendh",
+    "t": "scores unpack layer",
+    "y": "par x u wc ws v",
+}
+ROUND = {
+    "v": "sum gather ge qx gend split eb npr cb boff pw fl cum places qt es qi ew mt qd p oc2 qn qp qo mn pick2 ms scatter "
+         "hold0' mw take0' mf step0' qv holdm hold1' take1' tn1' takem qh step1' hold2' tn2' take2' srf step2' hold3' holds tn3' "
+         "take3' isroot takes step3'",
+    "s": "gather upper dx dp p vals own picks2 pf double0' opf relu tm1' double1' srf0 tm2' double2' tm3' xm",
+    "g": "send sendh",
+    "t": "back scores unpack layer",
+    "y": "op",
+}
+LAST = {"v": "sum gather qx y", "s": "gather scales y", "g": "", "t": "back y", "y": "oc scales"}
 
 
 def sb(n, d):
@@ -23,19 +40,19 @@ SCRATCH = {
     "uq": sb(128, FP8), "us": sb(128, U8), "vq": sb(128, FP8), "vs": sb(128, U8),
     "upq": sb(384, FP8), "ups": sb(384, U8), "eq": sb(512, FP8), "es": sb(512, U8),
     "lq": sb(C + 5 * A, FP8), "ls": sb(C + 5 * A, U8), "oq": sb(6 * 128, FP8), "osn": sb(6 * 128, U8),
-    "rq": sb(6 * A, FP8), "rs": sb(6 * 256, U8), "gq": sb(C, FP8), "gs": sb(C, U8), "gl": sb(8, U16),
-    "fq": sb(C, FP8), "fs": sb(C, U8), "fo": sb(8, U16),
+    "rq": sb(6 * A, FP8), "rs": sb(6 * A, U8), "gq": sb(C, FP8), "gs": sb(C, U8), "fq": sb(C, FP8), "fs": sb(C, U8),
     "xq1": sb(C, FP8), "xs1": sb(C, U8), "xq2": sb(C, FP8), "xs2": sb(C, U8), "xq3": sb(C, FP8), "xs3": sb(C, U8),
-    "pi": sb(2, I32), "ci": sb(8, I32), "cf": sb(8, F32), "cf1": sb(8, F32), "cd": sb(12, F32),
+    "pwu": sb(12, U16), "gp": sb(12, U16), "fp": sb(12, U16), "ew0": sb(4, U16), "gl": sb(4, U16), "fo": sb(4, U16),
+    "pi": sb(1, I32), "ci": sb(5, I32), "cf": sb(9, F32), "cd": sb(10, F32),
     "iot": sb(W + C, BF), "jm16": sb(C, BF), "kap": sb(C, BF), "zt": sb(520, BF),
-    "ti": sb(128, F32), "tj": sb(128, F32), "oc16": sb(36, U16), "osm": sb(8, U16),
+    "ti": sb(128, F32), "tj": sb(128, F32), "oc16": sb(24, U16), "osm": sb(4, U16),
     "h16": sb(C, BF), "ha": sb(C, BF), "hb": sb(C, BF), "cap": sb(C, F32), "ge0": sb(C, BF), "ge": sb(C, BF), "m1": sb(C, BF),
     "w1": sb(12, U16), "w2": sb(12, U16), "w4": sb(12, U16), "w8": sb(12, U16),
-    "p1": sb(384, BF), "p2": sb(C, BF), "p4": sb(C, BF), "p8": sb(C, BF), "sc": sb(C, BF),
+    "p1": sb(384, BF), "p2": sb(C, BF), "p4": sb(C, BF), "p8": sb(C, BF), "sc": sb(C, BF), "rootf": sb(C, BF),
     "im": sb(C, BF), "inn": sb(C, BF), "ta": sb(C, BF), "tm": sb(C, BF), "tn": sb(C, BF), "t2a": sb(C, F32), "tw": sb(392, F32),
     "eb": sb(C, F32), "npr": sb(C, BF), "cb": sb(C, BF), "boff": sb(2, U16), "pw": sb(32, U16), "pf": sb(272, BF),
-    "fl": sb(C, BF), "cum": sb(264, BF), "rootf": sb(C, BF), "vl": sb(34, F32), "rr": sb(34, F32), "es1": sb(32, F32),
-    "ew": sb(4, U16), "slf": sb(A, BF), "sls": sb(A, BF), "slo": sb(8, U16), "pws": sb(C, BF), "pwr": sb(16, F32),
+    "fl": sb(C, BF), "cum": sb(256, BF), "vl": sb(34, F32), "rr": sb(34, F32), "es1": sb(32, F32), "ew": sb(4, U16),
+    "pws": sb(C, BF), "pwr": sb(16, F32), "vals": sb(C + 1, BF),
     "m_t": sb(32, F32), "m_n": sb(32, F32), "m_s": sb(32, F32), "mw": sb(4, U16), "mf": sb(A, BF), "ms": sb(A, BF),
     "mo": sb(4, U16), "srf": sb(W, BF), "srs": sb(C, BF), "sro": sb(12, U16),
     "q_t": sb(16, F32), "q_i": sb(16, F32), "q_d": sb(16, F32), "q_o": sb(16, F32), "qo": sb(12, U16),
@@ -43,7 +60,7 @@ SCRATCH = {
 }
 LOADS = ["par", "x", "u", "wc", "ws", "v"]
 STORES = ["y", "op", "oc", "s0", "s1", "s2", "s3"]
-SEMAPHORES = (["cv", "cs", "ct", "cg", "lo", "ral", "lal"] + ["d_" + n for n in LOADS + STORES]
+SEMAPHORES = (["cv", "cs", "ct", "cg", "lo", "ral", "lal", "rap", "lap"] + ["d_" + n for n in LOADS + STORES]
               + ["ra%d" % s for s in range(6)] + ["la%d" % s for s in range(6)])
 
 
@@ -70,72 +87,27 @@ def helper_program(g, core, T, topo, rank, which):
     every = len(topo.engines(T.cores[rank], core))
     sent = [0]
 
-    def hand(out, src, came, k, lands, dst):
+    def hand(out, src, came, lands, dst):
         rid, pid = topo.addr(dst, core)
-        g.wait_ge(T.sem[came], k)
+        g.wait_ge(T.sem[came], every)
         g.remote_dma(out, src, T.sem[lands], T.sem.lo, pid, rid, topo.mask(core, dst))
         sent[0] += len(topo.engines(core, dst))
 
     dst = T.cores[rank ^ STEP[0]]
     if which == 0:
-        hand(T.fq[:].bitcast(dt.uint8), T.gq[:].bitcast(dt.uint8), "ra0", every // 2, "la0", dst)
+        hand(T.fq[:].bitcast(dt.uint8), T.gq[:].bitcast(dt.uint8), "ra0", "la0", dst)
     else:
-        hand(T.fs[:], T.gs[:], "ra0", every // 2, "la0", dst)
-        hand(T.fo[:], T.gl[:], "ral", every, "lal", dst)
+        hand(T.fs[:], T.gs[:], "ra0", "la0", dst)
+        hand(T.fp[:], T.gp[:], "rap", "lap", dst)
+        hand(T.fo[:], T.gl[:], "ral", "lal", dst)
     for s in range(1, 6):
         lo = landing(s)
         if which == 0:
             src, out = T.rq[:, A * s:A * s + A].bitcast(dt.uint8), T.lq[:, lo:lo + A].bitcast(dt.uint8)
         else:
-            a = 256 * s + 128 + live(s)
-            src, out = T.rs[:, a:a + A], T.ls[:, lo:lo + A]
-        hand(out, src, "ra%d" % s, every // 2, "la%d" % s, T.cores[rank ^ STEP[s // 2]])
+            src, out = T.rs[:, A * s:A * s + A], T.ls[:, lo:lo + A]
+        hand(out, src, "ra%d" % s, "la%d" % s, T.cores[rank ^ STEP[s // 2]])
     g.wait_ge(T.sem.lo, sent[0])
-
-
-def plan(calls):
-    n = len(calls)
-    back = [[] for c in calls]
-    for i, c in enumerate(calls):
-        for d in c[3]:
-            back[n - 1 - d].append(n - 1 - i)
-    end = one_pass(calls, None)[1]
-    end = one_pass([calls[n - 1 - i][:3] + (back[i],) for i in range(n)], end[::-1])[1]
-    return one_pass(calls, end[::-1])[0]
-
-
-def one_pass(calls, given):
-    n = len(calls)
-    behind = [[] for c in calls]
-    for i, c in enumerate(calls):
-        for d in c[3]:
-            behind[d].append(i)
-    way = [0.0] * n
-    for i in reversed(range(n)):
-        way[i] = calls[i][1] + max([WAKE + way[j] for j in behind[i]], default=0.0)
-    way = given or way
-    end, free, order, todo = {}, {}, [], list(range(n))
-    while todo:
-        soonest = {}
-        for k in todo:
-            ready = max([(end[d] if d in end else soonest[d] + calls[d][1]) + WAKE for d in calls[k][3]], default=0.0)
-            soonest[k] = max(ready, free.get(calls[k][0], 0.0))
-        top = max(soonest[k] + way[k] for k in todo)
-        latest = {k: soonest[k] + ALLOW + SLACK * (top - soonest[k] - way[k]) for k in todo}
-        can = sorted((k for k in todo if all(d in end for d in calls[k][3])), key=lambda k: (soonest[k], -way[k]))
-
-        def done(i):
-            return soonest[i] + (calls[i][1] if calls[i][2] else ISSUE)
-
-        fits = [i for i in can if calls[i][0] is None
-                or not any(calls[k][0] == calls[i][0] and way[k] > way[i] and latest[k] < done(i) for k in todo)]
-        i = fits[0] if fits else max(can, key=lambda k: way[k])
-        end[i] = soonest[i] + calls[i][1]
-        if calls[i][0] is not None:
-            free[calls[i][0]] = done(i)
-        order.append(i)
-        todo.remove(i)
-    return order, [end[i] for i in range(n)]
 
 
 def rank_program(g, core, T, topo):
@@ -150,6 +122,7 @@ def rank_program(g, core, T, topo):
     Q = {"v": g.vector, "s": g.scalar, "t": g.tensor, "g": g, "y": g.sync}
     CNT = {"v": "cv", "s": "cs", "t": "ct", "g": "cg"}
     ops = []
+    part = [0]
     left = {}
     touched = {}
 
@@ -164,6 +137,10 @@ def rank_program(g, core, T, topo):
 
     def plane(name, b, width=W, lo=0, hi=None):
         return B(name, width * b + lo, width * b + (width if hi is None else hi))
+
+    def width(v):
+        name, lo, hi, step = v[1][0]
+        return -((lo - hi) // step)
 
     def ind(win, off):
         return (win[0].indirect(off[0]), win[1], off[1])
@@ -186,27 +163,7 @@ def rank_program(g, core, T, topo):
                 seen[:] = [e for e in seen if not (step == 1 and lo <= e[0] and e[1] <= hi)]
             seen.append((lo, hi, step, me, writes))
 
-    def width(v):
-        name, lo, hi, step = (v[2] if len(v) > 2 else v[1])[0]
-        return 16 * (hi - lo) if len(v) > 2 else -((lo - hi) // step)
-
-    def cost(q, outs, ins):
-        views = [v for v in ins if isinstance(v, tuple)]
-        wide = [v for v in views if width(v) > 1]
-        n = width(outs[0])
-        if len(outs[0]) > 2:
-            return FIXED + SCATTER * CYCLE * n
-        if any(len(v) > 2 for v in views):
-            return FIXED + GATHER * CYCLE * n
-        if q == "g":
-            return 2 * FIXED + 2 * CYCLE * n
-        if q == "t":
-            return CYCLE * (width(views[2]) + 16)
-        if q == "v" and len(wide) < 2 and all(SCRATCH[v[1][0][0]][2] in (BF, U16) for v in wide + outs):
-            n = n // 2
-        return max(FIXED, CYCLE * n)
-
-    def add(q, call, outs, ins, sem=None, time=None, after=()):
+    def add(n, q, call, outs, ins, sem=None, after=()):
         me, deps = len(ops), []
         for v in ins:
             if isinstance(v, tuple):
@@ -215,11 +172,11 @@ def rank_program(g, core, T, topo):
             if len(v) > 2:
                 note(me, v[2], False, deps)
             note(me, v[1], True, deps)
-        ops.append([q, call, deps, sem, False, cost(q, outs, ins) if time is None else time, list(after)])
+        ops.append([q, call, deps, sem, False, (part[0], n), list(after)])
 
-    def arrival(name, t, which, *views):
+    def arrival(sem, t, which, *views):
         far = helpers(T, rank ^ STEP[t], topo)
-        add(None, None, list(views), [], (name, sum(len(topo.engines(far[k], core)) for k in which)), *left["r" + name[1:]])
+        add(sem, None, None, list(views), [], (sem, sum(len(topo.engines(far[k], core)) for k in which)), left["r" + sem[1:]])
 
     def a_(v):
         return v[0] if isinstance(v, tuple) else v
@@ -227,87 +184,73 @@ def rank_program(g, core, T, topo):
     O = AluOpType
     IDENT = ActivationFunctionType.Identity
 
-    def copy(out, in_):
-        add("v", lambda: g.vector.tensor_copy(out[0], in_[0]), [out], [in_])
+    def copy(n, out, in_):
+        add(n, "v", lambda: g.vector.tensor_copy(out[0], in_[0]), [out], [in_])
 
-    def tt(out, x, y, op):
-        add("v", lambda: g.vector.tensor_tensor(out[0], x[0], y[0], op), [out], [x, y])
+    def tt(n, out, x, y, op):
+        add(n, "v", lambda: g.vector.tensor_tensor(out[0], x[0], y[0], op), [out], [x, y])
 
-    def ts(out, x, s1, op0, s2=None, op1=None):
+    def ts(n, out, x, s1, op0, s2=None, op1=None):
         if op1 is None:
-            add("v", lambda: g.vector.tensor_scalar(out[0], x[0], a_(s1), None, op0), [out], [x, s1])
+            add(n, "v", lambda: g.vector.tensor_scalar(out[0], x[0], a_(s1), None, op0), [out], [x, s1])
         else:
-            add("v", lambda: g.vector.tensor_scalar(out[0], x[0], a_(s1), a_(s2), op0, op1), [out], [x, s1, s2])
+            add(n, "v", lambda: g.vector.tensor_scalar(out[0], x[0], a_(s1), a_(s2), op0, op1), [out], [x, s1, s2])
 
-    def scan(out, d0, d1, init, op0, op1):
-        add("v", lambda: g.vector.tensor_tensor_scan(out[0], d0[0], d1[0], init, op0, op1), [out], [d0, d1])
+    def scan(n, out, d0, d1, init, op0, op1):
+        add(n, "v", lambda: g.vector.tensor_tensor_scan(out[0], d0[0], d1[0], init, op0, op1), [out], [d0, d1])
 
-    def fill(out, c):
-        add("v", lambda: g.vector.memset(out[0], c), [out], [])
+    def fill(n, out, c):
+        add(n, "v", lambda: g.vector.memset(out[0], c), [out], [])
 
-    def quant(q, s, x):
-        add("v", lambda: g.vector.quantize_mx(q[0], s[0], x[0]), [q, s], [x])
+    def quant(n, q, s, x):
+        add(n, "v", lambda: g.vector.quantize_mx(q[0], s[0], x[0]), [q, s], [x])
 
-    def lin(out, in_, scale, bias):
-        add("s", lambda: g.scalar.activation(out[0], in_[0], IDENT, bias=a_(bias), scale=a_(scale)), [out], [in_, scale, bias])
+    def lin(n, out, in_, scale, bias):
+        add(n, "s", lambda: g.scalar.activation(out[0], in_[0], IDENT, bias=a_(bias), scale=a_(scale)), [out], [in_, scale, bias])
 
-    def act(out, in_, func=ActivationFunctionType.Copy, scale=None):
+    def act(n, out, in_, func=ActivationFunctionType.Copy, scale=None):
         if scale is None:
-            add("s", lambda: g.scalar.activation(out[0], in_[0], func), [out], [in_])
+            add(n, "s", lambda: g.scalar.activation(out[0], in_[0], func), [out], [in_])
         else:
-            add("s", lambda: g.scalar.activation(out[0], in_[0], func, scale=a_(scale)), [out], [in_, scale])
+            add(n, "s", lambda: g.scalar.activation(out[0], in_[0], func, scale=a_(scale)), [out], [in_, scale])
 
-    def move(q, out, in_):
-        (copy if q == "v" else act)(out, in_)
+    def move(n, q, out, in_):
+        (copy if q == "v" else act)(n, out, in_)
 
-    def times(q, out, in_, c):
-        if q == "v":
-            ts(out, in_, c, O.mult)
-        else:
-            act(out, in_, IDENT, c)
-
-    def mm(bank, w, lq_, ls_, rq_, rs_):
+    def mm(n, bank, w, lq_, ls_, rq_, rs_):
         out = B("ps", 512 * bank, 512 * bank + w)
-        add("t", lambda: g.tensor.matmul_mx(out[0], lq_[0], ls_[0], rq_[0], rs_[0], True, True),
+        add(n, "t", lambda: g.tensor.matmul_mx(out[0], lq_[0], ls_[0], rq_[0], rs_[0], True, True),
             [B("ps", 512 * bank, 512 * bank + 512)], [lq_, ls_, rq_, rs_])
 
-    def iota(out, pattern, base, cm, whole=False):
+    def iota(n, out, pattern, base, cm=0, whole=False):
         if whole:
-            add("g", lambda: g.iota(out[0], pattern, base, cm), [out], [])
+            add(n, "g", lambda: g.iota(out[0], pattern, base, cm), [out], [])
         else:
-            add("g", lambda: g.iota(out[0], pattern, base, cm, allow_small_or_imprecise_dtypes=True), [out], [])
+            add(n, "g", lambda: g.iota(out[0], pattern, base, cm, allow_small_or_imprecise_dtypes=True), [out], [])
 
-    def dma(q, name, out, in_, outs, ins):
-        add(q, lambda: Q[q].dma_start(out, in_), outs, ins, ("d_" + name, 16), LOAD.get(name, 1.2))
+    def dma(n, q, sem, out, in_, outs, ins):
+        add(n, q, lambda: Q[q].dma_start(out, in_), outs, ins, ("d_" + sem, 16))
 
     eng = topo.engines(core, hs[0])
-    half = len(eng) // 2
-    (r0, p0), (r1, p1) = topo.addr(hs[0], core), topo.addr(hs[1], core)
+    near = [topo.addr(h, core) for h in hs]
 
-    def write(out, src, view, sem, pid, rid, engines):
-        add("g", lambda: g.remote_dma(out, src, T.sem[sem], T.sem.lo, pid, rid, bits(engines)), [], [view],
-            ("lo", len(engines)), ISSUE)
-        left.setdefault(sem, (FIRST_CROSSING if sem == "ra0" else CROSSING, []))[1].append(len(ops) - 1)
+    def write(n, which, out, src, view, sem):
+        rid, pid = near[which]
+        add(n, "g", lambda: g.remote_dma(out, src, T.sem[sem], T.sem.lo, pid, rid, bits(eng)), [], [view], ("lo", len(eng)))
+        left.setdefault(sem, []).append(len(ops) - 1)
 
-    def send(s):
-        base = 128 * s
-        cq = B("oq", base + live(s), base + live(s) + A)
-        cs = B("osn", base - 128, base + 128)
-        sem = T.sem["ra%d" % s]
-        add("g", lambda: g.remote_dma_fused([
-            RemoteDMATransfer(dst_ids=[DstId(rid=r0, pnc=p0)], dma_engine_mask=bits(eng[:half]), remote_sem=sem,
-                              src=cq[0].bitcast(dt.uint8), dst=T.rq[:, A * s:A * s + A].bitcast(dt.uint8)),
-            RemoteDMATransfer(dst_ids=[DstId(rid=r1, pnc=p1)], dma_engine_mask=bits(eng[half:]), remote_sem=sem,
-                              src=cs[0], dst=T.rs[:, 256 * s:256 * s + 256]),
-        ], local_sem=T.sem.lo), [], [cq, cs], ("lo", 2 * half), ISSUE)
-        left["ra%d" % s] = (CROSSING, [len(ops) - 1])
+    def send(n, s):
+        lo = 128 * s + live(s)
+        cq, cs = B("oq", lo, lo + A), B("osn", lo, lo + A)
+        write(n, 0, T.rq[:, A * s:A * s + A].bitcast(dt.uint8), cq[0].bitcast(dt.uint8), cq, "ra%d" % s)
+        write(n, 1, T.rs[:, A * s:A * s + A], cs[0], cs, "ra%d" % s)
 
-    def hold(tmp, free, n):
-        scan(B(tmp, 0, n), B("h16", 0, n), free, 0.0, O.add, O.min)
+    def take(n, out, tmp, k):
+        ts(n, out, B(tmp, 15, k, 16), col("cd", 4), O.add)
 
-    def wrap(out, free, tmp, n):
-        hold(tmp, free, n)
-        ts(out, B(tmp, 15, n, 16), col("cd", 4), O.add)
+    def wrap(mark, out, free, tmp, k):
+        scan("hold" + mark, B(tmp, 0, k), B("h16", 0, k), free, 0.0, O.add, O.min)
+        take("take" + mark, out, tmp, k)
 
     IDS = B("iot", 0, C)
     PF = B("pf", 16, 272)
@@ -318,74 +261,77 @@ def rank_program(g, core, T, topo):
     def xcodes(t):
         return (B("lq", 0, C), B("ls", 0, C)) if t == 0 else (B("xq%d" % t), B("xs%d" % t))
 
-    def unpack(w, q, s):
+    def unpack(n, w, q, s):
         for b in range(4):
-            mm(b, w, B("eq", 128 * b, 128 * b + 128), B("es", 128 * b, 128 * b + 128), q, s)
+            mm(n, b, w, B("eq", 128 * b, 128 * b + 128), B("es", 128 * b, 128 * b + 128), q, s)
+
+    def planes_of_d():
+        for b in range(4):
+            act("dx", plane("dx", b, C), B("ps", 512 * b, 512 * b + C))
+
+    def along_paths(paths, queues):
+        for b, q in enumerate(queues):
+            move("dp", q, plane("dp", b, hi=C), ind(plane("dx", b, C), paths))
 
     def tables(first):
         levels = [("p1", "w1"), ("p2", "w2"), ("p4", "w4"), ("p8", "w8")]
         for lv, (p, w) in enumerate(levels):
+            mark = str(lv) + ("" if first else "'")
             if lv > 0 or not first:
-                wrap(B(w), B(p, 0, C), "sc", C)
+                wrap(mark, B(w), B(p, 0, C), "sc", C)
             if lv < 3:
-                act(B(levels[lv + 1][0]), ind(B(p, 0, C), B(w)))
+                act("double" + mark, B(levels[lv + 1][0]), ind(B(p, 0, C), B(w)))
             if lv > 0:
-                times("s", B("tm"), B("ta"), col("cf", 1 + lv))
-                times("v", B("tn"), B("ta"), col("cd", lv))
+                act("tm" + mark, B("tm"), B("ta"), IDENT, col("cf", 1 + lv))
+                ts("tn" + mark, B("tn"), B("ta"), col("cd", lv), O.mult)
             m, n = ("tm", "tn") if lv else ("im", "inn")
-            tt(B("ta") if lv < 3 else B("tw", 0, C), ind(B(m), B(w)), B(n), O.add)
-        if first:
-            act(B("iot", W, W + C), ind(B("p8"), B("w8")))
-        else:
-            act(B("t2a"), ind(B("tw", 0, C), B("w8")))
-            act(B("tw", C, 2 * C), ind(B("t2a"), B("w8")))
+            tt("step" + mark, B("ta") if lv < 3 else B("tw", 0, C), ind(B(m), B(w)), B(n), O.add)
 
     def best(t):
-        mm(4, C, B("upq", 128 * t, 128 * t + 128), B("ups", 128 * t, 128 * t + 128), *xcodes(t))
-        scan(B("eb", 1, C), B("ps", 2048, 2048 + C - 1), B("cap", 1, C), -BIG, O.max, O.min)
-        tt(B("npr"), B("ps", 2048, 2048 + C), B("eb"), O.is_le)
-        scan(B("cb"), B("npr"), B("ge" if t else "ge0"), 0.0, O.min, O.add)
-        ts(BEST, col("cb", C - 1), -64.0, O.mult, col("cd", 8 if t else 5), O.add)
+        mm("scores", 4, C, B("upq", 128 * t, 128 * t + 128), B("ups", 128 * t, 128 * t + 128), *xcodes(t))
+        scan("eb", B("eb", 1, C), B("ps", 2048, 2048 + C - 1), B("cap", 1, C), -BIG, O.max, O.min)
+        tt("npr", B("npr"), B("ps", 2048, 2048 + C), B("eb"), O.is_le)
+        scan("cb", B("cb"), B("npr"), B("ge" if t else "ge0"), 0.0, O.min, O.add)
+        ts("boff", BEST, col("cb", C - 1), -64.0, O.mult, col("cd", 8 if t else 5), O.add)
 
-    def places():
-        tt(B("vl", 1, 33), ind(B("cum"), OS), B("tj", 0, 32), O.is_ge)
-        tt(B("rr", 1, 33), ind(B("cum"), OS), B("tj", 32, 64), O.add)
-        scan(B("es1"), B("vl", 0, 32), B("rr", 1, 33), 0.0, O.mult, O.max)
-        copy(B("ew"), B("es1", 7, 32, 8))
+    def places(out):
+        tt("places", B("vl", 1, 33), ind(B("cum"), OS), B("tj", 0, 32), O.is_ge)
+        tt("places", B("rr", 1, 33), ind(B("cum"), OS), B("tj", 32, 64), O.add)
+        scan("es", B("es1"), B("vl", 0, 32), B("rr", 1, 33), 0.0, O.mult, O.max)
+        copy("ew", B(out), B("es1", 7, 32, 8))
 
     def new_parents(t):
-        tt(B("q_t"), ind(B("cum"), col("osm", 4)), B("tj", 96, 112), O.subtract)
-        tt(B("q_i"), ind(B("cum"), col("osm", 2)), B("q_t"), O.is_le)
-        tt(B("q_d"), B("q_i"), B("tj", 112, 128), O.mult)
+        tt("qt", B("q_t"), ind(B("cum", 32), col("osm", 2)), B("tj", 96, 112), O.subtract)
+        tt("qi", B("q_i"), ind(B("cum"), col("osm", 2)), B("q_t"), O.is_le)
+        tt("qd", B("q_d"), B("q_i"), B("tj", 112, 128), O.mult)
         if t == 0:
-            act(B("rootf", 0, C, 32), B("pf", 47, 47 + C, 32))
-            wrap(B("pwr", 0, 12), B("pf", 16, 16 + C), "pws", C)
-            tt(B("q_o", 0, 12), B("pwr", 0, 12), B("q_d", 0, 12), O.max)
+            take("pwr", B("pwr", 0, 12), "pws", C)
+            tt("qn", B("q_o", 0, 12), B("pwr", 0, 12), B("q_d", 0, 12), O.max)
         else:
-            tt(B("q_o"), ind(B("tw"), BEST), B("q_d"), O.max)
-        copy(B("qo"), B("q_o", 0, 12))
-        copy(B("pf", 15, 15 + C, 32), B("pf", 16, 16 + C, 32))
-        copy(ind(B("p1"), B("qo")), B("pf", 15, 15 + C))
-        copy(B("pf", 47, 47 + C, 32), B("rootf", 0, C, 32))
+            tt("qn", B("q_o"), ind(B("tw"), BEST), B("q_d"), O.max)
+        copy("qo", B("qo"), B("q_o", 0, 12))
+        act("vals", B("vals", 1, C + 1), ind(B("iot"), PW))
+        act("own", B("vals", 0, C, 32), B("vals", 1, C, 32))
+        copy("scatter", ind(B("p1"), B("qo")), B("vals", 0, C))
 
     def mirror(t):
-        tt(B("m_t"), B("rr", 0, 32), B("ti", 64, 96), O.subtract)
-        tt(B("m_n"), B("m_t"), B("tj", 64, 96), O.max)
-        scan(B("m_s"), B("vl", 0, 32), B("m_n"), 0.0, O.mult, O.min)
-        ts(B("mw"), B("m_s", 7, 32, 8), -1.0, O.mult)
-        copy(B("mf"), ind(PF, B("mw")))
-        wrap(B("mo"), B("mf"), "ms", A)
-        act(B("srf"), B("iot", 0, W))
-        copy(ind(B("srf"), B("mo")), B("iot", C, W))
-        wrap(B("sro"), B("srf", 0, C), "srs", C)
+        tt("mt", B("m_t"), B("rr", 0, 32), B("ti", 64, 96), O.subtract)
+        tt("mn", B("m_n"), B("m_t"), B("tj", 64, 96), O.max)
+        scan("ms", B("m_s"), B("vl", 0, 32), B("m_n"), 0.0, O.mult, O.min)
+        ts("mw", B("mw"), B("m_s", 7, 32, 8), -1.0, O.mult)
+        copy("mf", B("mf"), ind(PF, B("mw")))
+        wrap("m", B("mo"), B("mf"), "ms", A)
+        act("srf0", B("srf"), B("iot", 0, W))
+        copy("srf", ind(B("srf"), B("mo")), B("iot", C, W))
+        wrap("s", B("sro"), B("srf", 0, C), "srs", C)
         for b in range(4):
-            copy(plane("xp", b, hi=C), B("xw%d" % t, b, 4 * C, 4))
-            act(plane("xm", b, A), ind(plane("xp", b), B("mo")))
+            copy("split", plane("xp", b, hi=C), B("xw%d" % t, b, 4 * C, 4))
+            act("xm", plane("xm", b, A), ind(plane("xp", b), B("mo")))
 
     def make_p(t, off, queues):
         for b, q in enumerate(queues):
-            move(q, B("ph", b, 4 * A, 4), ind(plane("dp", b), B(off, 0, 4)))
-        quant(B("oq", 256 * t, 256 * t + 128), B("osn", 256 * t, 256 * t + 128), B("ph", 0, 512))
+            move("p", q, B("ph", b, 4 * A, 4), ind(plane("dp", b), B(off, 0, 4)))
+        quant("qp", B("oq", 256 * t, 256 * t + 128), B("osn", 256 * t, 256 * t + 128), B("ph", 0, 512))
 
     def layer(t):
         s = 2 * t
@@ -396,168 +342,185 @@ def rank_program(g, core, T, topo):
             arrival("la%d" % s, t, [0, 1], B("lq", lo, lo + A), B("ls", lo, lo + A))
             pq, psc, at = B("lq", lo - A, lo + A), B("ls", lo - A, lo + A), A
         for b in range(4):
-            mm(4 + b, 128, B("wq", 128 * b, 128 * b + 128), B("wsc", 128 * b, 128 * b + 128), pq, psc)
+            mm("layer", 4 + b, 128, B("wq", 128 * b, 128 * b + 128), B("wsc", 128 * b, 128 * b + 128), pq, psc)
         for b in range(4):
             lo = 512 * (4 + b) + at
-            act(B("ph", 512 + b, 768, 4), B("ps", lo, lo + A), ActivationFunctionType.Relu, 0.03125)
+            act("relu", B("ph", 512 + b, 768, 4), B("ps", lo, lo + A), ActivationFunctionType.Relu, 0.03125)
         base = 128 * (s + 1)
-        quant(B("oq", base, base + 128), B("osn", base, base + 128), B("ph", 256, 768))
-        send(s + 1)
+        quant("qh", B("oq", base, base + 128), B("osn", base, base + 128), B("ph", 256, 768))
+        send("sendh", s + 1)
 
     def update(t):
+        part[0] = t + 1
         lo = landing(2 * t + 1)
         arrival("la%d" % (2 * t + 1), t, [0, 1], B("lq", lo, lo + A), B("ls", lo, lo + A))
-        unpack(128, B("lq", lo - A, lo + A), B("ls", lo - A, lo + A))
+        unpack("back", 128, B("lq", lo - A, lo + A), B("ls", lo - A, lo + A))
         nx = "xw%d" % (t + 1)
         for b in range(4):
-            tt(plane("xp", b, lo=C), B("ps", 512 * b + A, 512 * b + 128), plane("xm", b, A), O.add)
+            tt("sum", plane("xp", b, lo=C), B("ps", 512 * b + A, 512 * b + 128), plane("xm", b, A), O.add)
         for q, b, c0, c1 in [("s", 0, 0, 12), ("s", 1, 0, 12), ("v", 2, 0, 12), ("v", 3, 0, 8), ("s", 3, 8, 12)]:
-            move(q, B(nx, 64 * c0 + b, 64 * c1, 4), ind(plane("xp", b), B("sro", c0, c1)))
-        xq, xs = xcodes(t + 1)
-        quant(xq, xs, B(nx))
+            move("gather", q, B(nx, 64 * c0 + b, 64 * c1, 4), ind(plane("xp", b), B("sro", c0, c1)))
+        quant("qx", *xcodes(t + 1), B(nx))
+        if t + 1 < R:
+            act("upper", B("t2a"), ind(B("tw", 0, C), B("w8")))
+            act("upper", B("tw", C, 2 * C), ind(B("t2a"), B("w8")))
 
     def rest(t):
         layer(t)
         new_parents(t)
         mirror(t)
         if t + 1 < R:
-            act(B("rootf"), ind(PF, B("oc16", 24, 36)))
+            tt("isroot", B("rootf"), B("p1", 0, C), IDS, O.is_equal)
             tables(False)
         else:
-            act(B("opf"), B("p1", 0, C))
-            dma("y", "op", T.op[:], T.opf[0:128:16, :], [], [B("opf")])
+            act("opf", B("opf"), B("p1", 0, C))
+            dma("op", "y", "op", T.op[:], T.opf[0:128:16, :], [], [B("opf")])
         update(t)
 
-    dma("y", "par", T.pari[:], T.par[:], [B("pari")], [])
-    dma("s", "x", T.xw0[:], T.x[:], [B("xw0")], [])
-    dma("y", "u", T.ub[:], T.u[:], [B("ub")], [])
-    dma("y", "wc", T.wq[:].bitcast(dt.uint8), T.wc[:], [B("wq")], [B("xw0"), B("ub")])
-    dma("y", "ws", T.wsc[:], T.ws[:], [B("wsc")], [B("xw0"), B("ub")])
-    dma("y", "v", T.vb[:], T.v[:], [B("vb")], [B("wq")])
+    dma("par", "y", "par", T.pari[:], T.par[:], [B("pari")], [])
+    dma("x", "y", "x", T.xw0[:], T.x[:], [B("xw0")], [])
+    dma("u", "y", "u", T.ub[:], T.u[:], [B("ub")], [])
+    dma("wc", "y", "wc", T.wq[:].bitcast(dt.uint8), T.wc[:], [B("wq")], [B("xw0"), B("ub")])
+    dma("ws", "y", "ws", T.wsc[:], T.ws[:], [B("wsc")], [B("xw0"), B("ub")])
+    dma("v", "y", "v", T.vb[:], T.v[:], [B("vb")], [B("wq")])
 
-    iota(col("pi", 0), [[0, 1]], 0, 1, True)
-    iota(B("iot", 0, W), [[1, W]], 0, 0)
-    iota(B("jm16"), [[0, 12], [1, 16]], 0, 0)
-    iota(B("kap"), [[1, 6], [0, 32]], 0, 0)
-    iota(B("ti", 0, 32), [[-16, 4], [-32, 8]], 224, 0)
-    iota(B("ti", 32, 64), [[16, 4], [0, 8]], 0, 0)
-    iota(B("ti", 64, 96), [[0, 4], [-64, 8]], 479, 0)
-    iota(B("ti", 96, 112), [[0, 8], [-16, 2]], 32, 0)
-    iota(B("ti", 112, 128), [[16, 16]], C, 0)
-    iota(B("zt", 512, 520), [[0, 8]], 0, 0)
-    iota(B("tw", 384, 392), [[0, 8]], 0, 0)
-    for b in range(4):
-        iota(plane("dp", b, lo=C), [[0, A]], 0, 0)
-        iota(plane("xp", b, lo=C), [[0, A]], 0, 0)
-    for view, c in [(B("ph", 256, 512), 0.0), (B("cap"), BIG), (B("cap", 0, C, 32), -BIG), (B("cum"), 0.0), (col("eb", 0), -BIG),
-                    (B("pf", 0, 16), -1.0), (col("vl", 0), 0.0), (col("rr", 0), 0.0), (B("slo", 4, 8), 0),
-                    (B("m1"), 0.0), (B("m1", 0, C, 32), -1.0)]:
-        fill(view, c)
-    for j, (sh, m) in enumerate([(0, 15), (0, 1), (1, 1), (2, 1), (3, 1), (1, 7), (0, 7), (0, 7)]):
-        ts(col("ci", j), col("pi", 0), sh, O.logical_shift_right, m, O.bitwise_and)
-    copy(B("cf"), B("ci"))
-    lin(B("cd", 0, 4), B("cf", 1, 5), -1.0, 1.0)
-    lin(B("cf1"), B("cf"), 1.0, 1.0)
-    ts(col("cd", 4), col("cf", 0), 15.0, O.is_lt, 256.0, O.mult)
-    ts(col("cd", 6), col("cf", 6), 6.0, O.min)
-    lin(col("cd", 5), col("cd", 6), 32.0, -32.0)
-    lin(col("cd", 7), col("cf", 5), 32.0, -32.0)
-    lin(col("cd", 8), col("cf", 1), float(C), col("cd", 7))
-    times("v", B("im"), IDS, col("cf", 1))
-    times("v", B("inn"), IDS, col("cd", 0))
-    ts(B("ha"), B("jm16"), col("cf", 0), O.is_le, 1280.0, O.mult)
-    ts(B("hb"), B("jm16"), col("cf1", 0), O.is_le, -256.0, O.mult)
-    tt(B("h16"), B("ha"), B("hb"), O.add)
-    for name, j in [("ge0", 6), ("ge", 5)]:
-        ts(B(name), B("kap"), col("cf", j), O.is_equal, 1.0 / 64, O.mult)
-        ts(B(name, 31, C, 32), B("kap", 31, C, 32), col("cf", j), O.is_equal, -63.0 / 64, O.mult)
-    ts(B("osm", 0, 2), B("cf", 6, 8), -32.0, O.mult, 224.0, O.add)
-    ts(col("osm", 2), col("cf", 5), 32.0, O.mult)
-    ts(col("osm", 4), col("cf1", 5), 32.0, O.mult)
-    ts(B("tj", 0, 32), B("ti", 0, 32), col("cf", 0), O.subtract)
-    lin(B("tj", 32, 64), B("ti", 32, 64), 1.0, col("cf", 0))
-    lin(B("tj", 64, 96), B("tj", 0, 32), -1.0, -63.0)
-    ts(B("tj", 96, 112), B("ti", 96, 112), col("cf", 0), O.subtract)
-    lin(B("tj", 112, 128), B("ti", 112, 128), 1.0, col("cf", 0))
-    act(B("pf", 16 + C, 272), B("iot", C, W))
-    for t in range(R):
-        ts(B("oc16", 8 * t, 8 * t + 8), B("iot", 0, 128, 16), float(t), O.add)
-    for h in (0, 1):
-        ts(B("oc16", 24 + h, 36, 2), B("iot", 0, C, 32), 0.0, O.add)
+    iota("pi", B("pi"), [[0, 1]], 0, 1, True)
+    fill("half", B("srf"), 0.5)
+    scan("iot", B("iot", 0, W), B("srf"), B("srf"), -1.0, O.add, O.add)
+    iota("jm16", B("jm16"), [[0, 12], [1, 16]], 0)
+    iota("kap", B("kap"), [[1, 6], [0, 32]], 0)
+    iota("ti0", B("ti", 0, 32), [[-16, 4], [-32, 8]], 224)
+    iota("ti0", B("ti", 32, 64), [[16, 4], [0, 8]], 0)
+    iota("ti64", B("ti", 64, 96), [[0, 4], [-64, 8]], 479)
+    iota("ti64", B("ti", 96, 112), [[0, 8], [-16, 2]], 32)
+    iota("ti64", B("ti", 112, 128), [[16, 16]], C)
+    for n, view, c in ([("tail", B("zt", 512, 520), 0), ("tw0", B("tw", 384, 392), 0), ("small", B("pf", 0, 16), -1),
+                        ("small", col("vl", 0), 0), ("small", col("rr", 0), 0), ("small", B("tw", C, C + 8), 0)]
+                       + [("dpz", plane("dp", b, lo=C), 0) for b in range(4)] + [("xpz", plane("xp", b, lo=C), 0) for b in range(4)]):
+        iota(n, view, [[0, width(view)]], c)
+    for n, view, c in [("zero", B("ph", 256, 512), 0.0), ("cum0", B("cum"), 0.0), ("eb0", col("eb", 0), -BIG),
+                       ("cap", B("cap"), BIG), ("capend", B("cap", 0, C, 32), -BIG),
+                       ("m1", B("m1"), 0.0), ("m1", B("m1", 0, C, 32), -1.0)]:
+        lin(n, view, B("iot", 0, width(view)), 0.0, c)
+    for j, (sh, m) in enumerate([(0, 15), (0, 1), (1, 1), (2, 1), (3, 1)]):
+        ts("ci", col("ci", j), col("pi", 0), sh, O.logical_shift_right, m, O.bitwise_and)
+    copy("cf", B("cf", 0, 5), B("ci"))
+    lin("q1", col("cf", 8), col("cf", 0), 1.0, 1.0)
+    for j in (6, 7):
+        lin("q8", col("cf", j), col("cf", 4), -8.0, col("cf", 0))
+    lin("q2", col("cd", 6), col("cf", 0), 0.5, 0.0)
+    lin("q2", col("cf", 5), col("cf", 1), -0.5, col("cd", 6))
+    lin("cd03", B("cd", 0, 4), B("cf", 1, 5), -1.0, 1.0)
+    ts("cd4", col("cd", 4), col("cf", 0), 15.0, O.is_lt, 256.0, O.mult)
+    lin("cd5", col("cd", 5), col("cf", 6), 32.0, -32.0)
+    lin("cd8", col("cd", 7), col("cf", 5), 32.0, -32.0)
+    lin("cd8", col("cd", 8), col("cf", 1), float(C), col("cd", 7))
+    lin("negq", col("cd", 9), col("cf", 0), -1.0, 0.0)
+    ts("im", B("im"), IDS, col("cf", 1), O.mult)
+    ts("inn", B("inn"), IDS, col("cd", 0), O.mult)
+    ts("ha", B("ha"), B("jm16"), col("cf", 0), O.is_le, 1024.0, O.mult)
+    ts("hb", B("hb"), B("jm16"), col("cf", 8), O.is_equal, -256.0, O.mult)
+    tt("h16", B("h16"), B("ha"), B("hb"), O.add)
+    ts("osm", B("osm", 0, 2), B("cf", 6, 8), -32.0, O.mult, 224.0, O.add)
+    ts("osm", col("osm", 2), col("cf", 5), 6.0, O.min, 32.0, O.mult)
+    lin("tj0", B("tj", 0, 32), B("ti", 0, 32), 1.0, col("cd", 9))
+    lin("tj32", B("tj", 32, 64), B("ti", 32, 64), 1.0, col("cf", 0))
+    lin("tj64", B("tj", 64, 96), B("tj", 0, 32), -1.0, -63.0)
+    lin("tj96", B("tj", 96, 112), B("ti", 96, 112), 1.0, col("cd", 9))
+    lin("tj112", B("tj", 112, 128), B("ti", 112, 128), 1.0, col("cf", 0))
+    act("sent", B("pf", 16 + C, 272), B("iot", C, W))
     for lo in (0, 256):
         out, zero = B("zt", lo, lo + 256), B("ph", 256, 512)
-        add("g", lambda out=out, zero=zero, lo=lo: g.affine_select(out[0], zero[0], [[1, 256]], O.not_equal, 1.0, lo - 3, -4),
-            [out], [zero])
+        add("unit%d" % (lo // 256), "g",
+            lambda out=out, zero=zero, lo=lo: g.affine_select(out[0], zero[0], [[1, 256]], O.not_equal, 1.0, lo - 3, -4), [out], [zero])
     for b in range(4):
-        quant(B("eq", 128 * b, 128 * b + 128), B("es", 128 * b, 128 * b + 128), B("zt", 3 - b, 515 - b))
-    quant(B("uq"), B("us"), B("ub"))
-    quant(B("vq"), B("vs"), B("vb"))
+        quant("eq%d" % b, B("eq", 128 * b, 128 * b + 128), B("es", 128 * b, 128 * b + 128), B("zt", 3 - b, 515 - b))
+    quant("qu", B("uq"), B("us"), B("ub"))
     for t in range(R):
+        part[0] = t // 2
         off = B("oc16", 8 * t, 8 * t + 8)
-        copy(w32(B("upq", 128 * t, 128 * t + 128)), ind(w32(B("uq")), off))
-        act(B("ups", 128 * t, 128 * t + 128), ind(B("us"), off))
+        ts("oc%d" % t, off, B("iot", 0, 128, 16), float(t), O.add)
+        copy("pick%d" % t, w32(B("upq", 128 * t, 128 * t + 128)), ind(w32(B("uq")), off))
+        act("picks%d" % t, B("ups", 128 * t, 128 * t + 128), ind(B("us"), off))
+    for t, n, j in [(0, "0", 6), (1, "", 5)]:
+        part[0] = t
+        ts("ge" + n, B("ge" + n), B("kap"), col("cf", j), O.is_equal, 1.0 / 64, O.mult)
+        ts("gend" + n, B("ge" + n, 31, C, 32), B("kap", 31, C, 32), col("cf", j), O.is_equal, -63.0 / 64, O.mult)
+    part[0] = 2
+    quant("qv", B("vq"), B("vs"), B("vb"))
+    part[0] = 0
 
-    quant(B("lq", 0, C), B("ls", 0, C), B("xw0"))
-    write(T.gq[:].bitcast(dt.uint8), T.lq[:, 0:C].bitcast(dt.uint8), B("lq", 0, C), "ra0", p0, r0, eng[:half])
-    write(T.gs[:], T.ls[:, 0:C], B("ls", 0, C), "ra0", p1, r1, eng[half:])
-    copy(B("w1"), B("pari"))
-    act(B("p1", 0, C), ind(IDS, B("w1")))
+    quant("qx", B("lq", 0, C), B("ls", 0, C), B("xw0"))
+    write("sendx", 0, T.gq[:].bitcast(dt.uint8), T.lq[:, 0:C].bitcast(dt.uint8), B("lq", 0, C), "ra0")
+    write("sendx", 1, T.gs[:], T.ls[:, 0:C], B("ls", 0, C), "ra0")
+    copy("w1", B("w1"), B("pari"))
+    act("p1", B("p1", 0, C), ind(IDS, B("w1")))
     tables(True)
+    act("p16", B("iot", W, W + C), ind(B("p8"), B("w8")))
     best(0)
-    copy(B("pw", 0, 32, 2), ind(B("tw", 0, C), BEST))
-    ts(B("pw", 1, 32, 2), ind(B("tw", 0, C), BEST), float(W), O.add)
-    copy(B("pf", 16, 16 + C // 2), ind(B("iot"), B("pw", 0, 6)))
-    act(B("pf", 16 + C // 2, 16 + C), ind(B("iot"), B("pw", 6, 12)))
-    tt(B("fl"), B("pf", 16, 16 + C), B("pf", 15, 15 + C), O.is_equal)
-    scan(B("cum", 1, C + 1), B("fl"), B("ph", 256, 256 + C), 0.0, O.add, O.add)
-    places()
-    copy(B("slf"), ind(PF, B("ew")))
-    wrap(B("slo", 0, 4), B("slf"), "sls", A)
-    write(T.gl[:], T.slo[:], B("slo"), "ral", p1, r1, eng)
+    copy("pw", B("pw", 0, 32, 2), ind(B("tw", 0, C + 8), BEST))
+    ts("pw", B("pw", 1, 32, 2), ind(B("tw", 0, C + 8), BEST), float(W), O.add)
+    copy("pf", B("pf", 16, 16 + C // 2), ind(B("iot"), B("pw", 0, 6)))
+    act("pf", B("pf", 16 + C // 2, 16 + C), ind(B("iot"), B("pw", 6, 12)))
+    wrap("p", B("pwu", 0, 12), B("pf", 16, 16 + C), "pws", C)
+    write("sendp", 1, T.gp[:], T.pwu[:], B("pwu"), "rap")
+    tt("fl", B("fl"), B("pf", 16, 16 + C), B("pf", 15, 15 + C), O.is_equal)
+    scan("cum", B("cum", 1, C + 1), B("fl"), B("ph", 256, 256 + C), 0.0, O.add, O.add)
+    places("ew0")
+    write("sende", 1, T.gl[:], T.ew0[:], B("ew0"), "ral")
     arrival("la0", 0, [0, 1], B("fq"), B("fs"))
-    unpack(C, B("fq"), B("fs"))
-    for b in range(4):
-        act(plane("dp", b, hi=C), B("ps", 512 * b, 512 * b + C))
+    unpack("unpack", C, B("fq"), B("fs"))
+    planes_of_d()
+    arrival("lap", 0, [1], B("fp"))
+    along_paths(B("fp", 0, 12), "svsv")
     arrival("lal", 0, [1], B("fo"))
     make_p(0, "fo", "vsvs")
     rest(0)
 
     for t in range(1, R):
         best(t)
-        unpack(C, *xcodes(t))
-        copy(B("pw", 0, 16), ind(B("tw"), BEST))
-        for b in range(4):
-            act(plane("dx", b, C), B("ps", 512 * b, 512 * b + C))
-        for b in range(4):
-            act(plane("dp", b, hi=C), ind(plane("dx", b, C), PW))
-        tt(B("fl"), ind(IDS, PW), B("rootf"), O.is_equal)
-        scan(B("cum", 1, C + 1), B("fl"), B("m1"), 0.0, O.add, O.add)
-        places()
-        make_p(t, "ew", "vvvs")
-        send(2 * t)
-        act(B("pf", 16, 16 + C), ind(IDS, PW))
+        unpack("unpack", C, *xcodes(t))
+        copy("pw", B("pw", 0, 16), ind(B("tw"), BEST))
+        planes_of_d()
+        along_paths(PW, "ssss")
+        copy("fl", B("fl"), ind(B("rootf"), PW))
+        scan("cum", B("cum", 1, C + 1), B("fl"), B("m1"), 0.0, O.add, O.add)
+        places("ew")
+        make_p(t, "ew", "vvss")
+        send("send", 2 * t)
+        act("pf", B("pf", 16, 16 + C), ind(IDS, PW))
         rest(t)
 
     xq, xs = xcodes(R)
-    mm(4, C, B("vq"), B("vs"), xq, xs)
-    dma("y", "oc", T.oc[:], xq[0].bitcast(dt.uint8), [], [xq])
+    mm("y", 4, C, B("vq"), B("vs"), xq, xs)
+    dma("oc", "y", "oc", T.oc[:], xq[0].bitcast(dt.uint8), [], [xq])
     for k in range(4):
-        dma("s" if k % 2 else "y", "s%d" % k, T.osc[4 * k:4 * k + 4, :], T.xs3[32 * k:32 * k + 4, :], [], [xs])
-    copy(B("yf"), B("ps", 2048, 2048 + C))
-    dma("s", "y", T.y[:], T.yf[:], [], [B("yf")])
+        dma("scales", "s" if k % 2 else "y", "s%d" % k, T.osc[4 * k:4 * k + 4, :], T.xs3[32 * k:32 * k + 4, :], [], [xs])
+    copy("y", B("yf"), B("ps", 2048, 2048 + C))
+    dma("y", "s", "y", T.y[:], T.yf[:], [], [B("yf")])
 
-    if not ORDER:
-        ORDER.extend(plan([(o[0], o[5], o[3] is None, sorted(set(o[2] + o[6]))) for o in ops]))
+    named, lines = {}, {None: [i for i, o in enumerate(ops) if o[0] is None]}
+    for i, o in enumerate(ops):
+        named.setdefault((o[0],) + o[5], []).append(i)
+    for q in Q:
+        lines[q] = [i for k, names in enumerate([FIRST, ROUND, ROUND, LAST]) for n in names[q].split() for i in named.get((q, k, n), [])]
+    order, out = [], set()
+    while len(order) < len(ops):
+        heads = [line for line in lines.values() if line and all(d in out for d in ops[line[0]][2] + ops[line[0]][6])]
+        assert heads
+        for line in heads:
+            order.append(line.pop(0))
+            out.add(order[-1])
     for o in ops:
         for d in o[2]:
             ops[d][4] = True
     token, total, waited = {}, {}, {}
-    for i in ORDER:
+    for i in order:
         o = ops[i]
         name, k = o[3] if o[3] else (CNT[o[0]], 1 if o[4] else 0)
         total[name] = total.get(name, 0) + k
         token[i] = (name, total[name])
-    for i in ORDER:
+    for i in order:
         q, call, deps, sem, needed = ops[i][:5]
         if q is None:
             continue

from concourse.mybir import dt, AluOpType, ActivationFunctionType

F32, BF, I32, U16, U8, FP8 = "float32", "bfloat16", "int32", "uint16", "uint8", "float8_e4m3fn_x4"
C, A, R = 192, 64, 3
W = C + A
STEP = [1, 2, 4]
BIG = 9.0e29

FIRST = {
    "v": "half iot ci cf w1 oc0 im ha hb inn cd4 h16 qx step0 hold1 qu tn1 take1 pick0 step1 ge0 oc1 hold2 eb take2 tn2 gend0 "
         "npr step2 hold3 cb tn3 take3 boff step3 pick1 pw eq0 pf osm fl holdp cum takep pwr places qt eq1 es qi mt ew qd eq3 mn "
         "qn eq2 qo ms scatter dp hold0' p take0' mw qp step0' mf hold1' split take1' tn1' qh holdm step1' takem hold2' isroot "
         "take2' tn2' srf step2' hold3' holds tn3' take3' takes step3'",
    "s": "zero cap q1 cd03 p1 negq double0 eb0 q8 capend sent tj112 tm1 picks0 double1 tm2 q2 cd5 double2 tm3 p16 pf cum0 tj32 "
         "tj0 tj96 cd8 vals srf0 own tj64 picks1 dx dp p double0' relu tm1' double1' m1 tm2' double2' tm3' xm",
    "g": "pi jm16 ti0 tail ti64 kap sendx unit1 tw0 unit0 small xpz sendp sende dpz sendh",
    "t": "scores unpack layer",
    "y": "par x u wc ws v",
}
ROUND = {
    "v": "sum gather ge qx gend split eb npr cb boff pw fl cum places qt es qi ew mt qd p oc2 qn qp qo mn pick2 ms scatter "
         "hold0' mw take0' mf step0' qv holdm hold1' take1' tn1' takem qh step1' hold2' tn2' take2' srf step2' hold3' holds tn3' "
         "take3' isroot takes step3'",
    "s": "gather upper dx dp p vals own picks2 pf double0' opf relu tm1' double1' srf0 tm2' double2' tm3' xm",
    "g": "send sendh",
    "t": "back scores unpack layer",
    "y": "op",
}
LAST = {"v": "sum gather qx y", "s": "gather scales y", "g": "", "t": "back y", "y": "oc scales"}


def sb(n, d):
    return ("sbuf", [128, n], d)


SCRATCH = {
    "ps": ("psum", [128, 4096], F32),
    "pari": sb(12, I32), "ub": sb(512, BF), "vb": sb(512, BF), "wq": sb(512, FP8), "wsc": sb(512, U8),
    "xw0": sb(4 * C, BF), "xw1": sb(4 * C, BF), "xw2": sb(4 * C, BF), "xw3": sb(4 * C, BF), "xp": sb(4 * W, BF),
    "uq": sb(128, FP8), "us": sb(128, U8), "vq": sb(128, FP8), "vs": sb(128, U8),
    "upq": sb(384, FP8), "ups": sb(384, U8), "eq": sb(512, FP8), "es": sb(512, U8),
    "lq": sb(C + 5 * A, FP8), "ls": sb(C + 5 * A, U8), "oq": sb(6 * 128, FP8), "osn": sb(6 * 128, U8),
    "rq": sb(6 * A, FP8), "rs": sb(6 * A, U8), "gq": sb(C, FP8), "gs": sb(C, U8), "fq": sb(C, FP8), "fs": sb(C, U8),
    "xq1": sb(C, FP8), "xs1": sb(C, U8), "xq2": sb(C, FP8), "xs2": sb(C, U8), "xq3": sb(C, FP8), "xs3": sb(C, U8),
    "pwu": sb(12, U16), "gp": sb(12, U16), "fp": sb(12, U16), "ew0": sb(4, U16), "gl": sb(4, U16), "fo": sb(4, U16),
    "pi": sb(1, I32), "ci": sb(5, I32), "cf": sb(9, F32), "cd": sb(10, F32),
    "iot": sb(W + C, BF), "jm16": sb(C, BF), "kap": sb(C, BF), "zt": sb(520, BF),
    "ti": sb(128, F32), "tj": sb(128, F32), "oc16": sb(24, U16), "osm": sb(4, U16),
    "h16": sb(C, BF), "ha": sb(C, BF), "hb": sb(C, BF), "cap": sb(C, F32), "ge0": sb(C, BF), "ge": sb(C, BF), "m1": sb(C, BF),
    "w1": sb(12, U16), "w2": sb(12, U16), "w4": sb(12, U16), "w8": sb(12, U16),
    "p1": sb(384, BF), "p2": sb(C, BF), "p4": sb(C, BF), "p8": sb(C, BF), "sc": sb(C, BF), "rootf": sb(C, BF),
    "im": sb(C, BF), "inn": sb(C, BF), "ta": sb(C, BF), "tm": sb(C, BF), "tn": sb(C, BF), "t2a": sb(C, F32), "tw": sb(392, F32),
    "eb": sb(C, F32), "npr": sb(C, BF), "cb": sb(C, BF), "boff": sb(2, U16), "pw": sb(32, U16), "pf": sb(272, BF),
    "fl": sb(C, BF), "cum": sb(256, BF), "vl": sb(34, F32), "rr": sb(34, F32), "es1": sb(32, F32), "ew": sb(4, U16),
    "pws": sb(C, BF), "pwr": sb(16, F32), "vals": sb(C + 1, BF),
    "m_t": sb(32, F32), "m_n": sb(32, F32), "m_s": sb(32, F32), "mw": sb(4, U16), "mf": sb(A, BF), "ms": sb(A, BF),
    "mo": sb(4, U16), "srf": sb(W, BF), "srs": sb(C, BF), "sro": sb(12, U16),
    "q_t": sb(16, F32), "q_i": sb(16, F32), "q_d": sb(16, F32), "q_o": sb(16, F32), "qo": sb(12, U16),
    "dx": sb(4 * C, BF), "dp": sb(4 * W, BF), "ph": sb(768, BF), "xm": sb(4 * A, BF), "yf": sb(C, F32), "opf": sb(C, F32),
}
LOADS = ["par", "x", "u", "wc", "ws", "v"]
STORES = ["y", "op", "oc", "s0", "s1", "s2", "s3"]
SEMAPHORES = (["cv", "cs", "ct", "cg", "lo", "ral", "lal", "rap", "lap"] + ["d_" + n for n in LOADS + STORES]
              + ["ra%d" % s for s in range(6)] + ["la%d" % s for s in range(6)])


def helpers(T, rank, topo):
    core = T.cores[rank]
    ok = [c for c in topo.cores_of(core) if c != core and all(topo.may_write(c, T.cores[rank ^ s]) for s in STEP)]
    ok.sort(key=lambda c: (topo.die(c) != topo.die(core), c))
    return ok[:2]


def bits(engines):
    return sum(1 << e for e in engines)


def live(s):
    return 0 if s % 2 == 0 else A


def landing(s):
    return C + A * (s - 1)


def helper_program(g, core, T, topo, rank, which):
    every = len(topo.engines(T.cores[rank], core))
    sent = [0]

    def hand(out, src, came, lands, dst):
        rid, pid = topo.addr(dst, core)
        g.wait_ge(T.sem[came], every)
        g.remote_dma(out, src, T.sem[lands], T.sem.lo, pid, rid, topo.mask(core, dst))
        sent[0] += len(topo.engines(core, dst))

    dst = T.cores[rank ^ STEP[0]]
    if which == 0:
        hand(T.fq[:].bitcast(dt.uint8), T.gq[:].bitcast(dt.uint8), "ra0", "la0", dst)
    else:
        hand(T.fs[:], T.gs[:], "ra0", "la0", dst)
        hand(T.fp[:], T.gp[:], "rap", "lap", dst)
        hand(T.fo[:], T.gl[:], "ral", "lal", dst)
    for s in range(1, 6):
        lo = landing(s)
        if which == 0:
            src, out = T.rq[:, A * s:A * s + A].bitcast(dt.uint8), T.lq[:, lo:lo + A].bitcast(dt.uint8)
        else:
            src, out = T.rs[:, A * s:A * s + A], T.ls[:, lo:lo + A]
        hand(out, src, "ra%d" % s, "la%d" % s, T.cores[rank ^ STEP[s // 2]])
    g.wait_ge(T.sem.lo, sent[0])


def rank_program(g, core, T, topo):
    rank = T.rank_of(core)
    if rank is None:
        for r in range(len(T.cores)):
            hs = helpers(T, r, topo)
            if core in hs:
                helper_program(g, core, T, topo, r, hs.index(core))
        return
    hs = helpers(T, rank, topo)
    Q = {"v": g.vector, "s": g.scalar, "t": g.tensor, "g": g, "y": g.sync}
    CNT = {"v": "cv", "s": "cs", "t": "ct", "g": "cg"}
    ops = []
    part = [0]
    left = {}
    touched = {}

    def B(name, lo=0, hi=None, step=1):
        if hi is None:
            hi = SCRATCH[name][1][1]
        ap = T[name][:, lo:hi] if step == 1 else T[name][:, lo:hi:step]
        return (ap, [(name, lo, hi, step)])

    def col(name, j):
        return B(name, j, j + 1)

    def plane(name, b, width=W, lo=0, hi=None):
        return B(name, width * b + lo, width * b + (width if hi is None else hi))

    def width(v):
        name, lo, hi, step = v[1][0]
        return -((lo - hi) // step)

    def ind(win, off):
        return (win[0].indirect(off[0]), win[1], off[1])

    def w32(v):
        return (v[0].bitcast(dt.uint32), v[1])

    def meet(a, b):
        if a[1] <= b[0] or b[1] <= a[0]:
            return False
        return not (a[2] == b[2] and a[2] > 1 and (a[0] - b[0]) % a[2])

    def note(me, regions, writes, deps):
        for name, lo, hi, step in regions:
            seen = touched.setdefault(name, [])
            for e in seen:
                if e[3] != me and (writes or e[4]) and meet((lo, hi, step), e):
                    deps.append(e[3])
            if writes:
                seen[:] = [e for e in seen if not (step == 1 and lo <= e[0] and e[1] <= hi)]
            seen.append((lo, hi, step, me, writes))

    def add(n, q, call, outs, ins, sem=None, after=()):
        me, deps = len(ops), []
        for v in ins:
            if isinstance(v, tuple):
                note(me, v[1] + (v[2] if len(v) > 2 else []), False, deps)
        for v in outs:
            if len(v) > 2:
                note(me, v[2], False, deps)
            note(me, v[1], True, deps)
        ops.append([q, call, deps, sem, False, (part[0], n), list(after)])

    def arrival(sem, t, which, *views):
        far = helpers(T, rank ^ STEP[t], topo)
        add(sem, None, None, list(views), [], (sem, sum(len(topo.engines(far[k], core)) for k in which)), left["r" + sem[1:]])

    def a_(v):
        return v[0] if isinstance(v, tuple) else v

    O = AluOpType
    IDENT = ActivationFunctionType.Identity

    def copy(n, out, in_):
        add(n, "v", lambda: g.vector.tensor_copy(out[0], in_[0]), [out], [in_])

    def tt(n, out, x, y, op):
        add(n, "v", lambda: g.vector.tensor_tensor(out[0], x[0], y[0], op), [out], [x, y])

    def ts(n, out, x, s1, op0, s2=None, op1=None):
        if op1 is None:
            add(n, "v", lambda: g.vector.tensor_scalar(out[0], x[0], a_(s1), None, op0), [out], [x, s1])
        else:
            add(n, "v", lambda: g.vector.tensor_scalar(out[0], x[0], a_(s1), a_(s2), op0, op1), [out], [x, s1, s2])

    def scan(n, out, d0, d1, init, op0, op1):
        add(n, "v", lambda: g.vector.tensor_tensor_scan(out[0], d0[0], d1[0], init, op0, op1), [out], [d0, d1])

    def fill(n, out, c):
        add(n, "v", lambda: g.vector.memset(out[0], c), [out], [])

    def quant(n, q, s, x):
        add(n, "v", lambda: g.vector.quantize_mx(q[0], s[0], x[0]), [q, s], [x])

    def lin(n, out, in_, scale, bias):
        add(n, "s", lambda: g.scalar.activation(out[0], in_[0], IDENT, bias=a_(bias), scale=a_(scale)), [out], [in_, scale, bias])

    def act(n, out, in_, func=ActivationFunctionType.Copy, scale=None):
        if scale is None:
            add(n, "s", lambda: g.scalar.activation(out[0], in_[0], func), [out], [in_])
        else:
            add(n, "s", lambda: g.scalar.activation(out[0], in_[0], func, scale=a_(scale)), [out], [in_, scale])

    def move(n, q, out, in_):
        (copy if q == "v" else act)(n, out, in_)

    def mm(n, bank, w, lq_, ls_, rq_, rs_):
        out = B("ps", 512 * bank, 512 * bank + w)
        add(n, "t", lambda: g.tensor.matmul_mx(out[0], lq_[0], ls_[0], rq_[0], rs_[0], True, True),
            [B("ps", 512 * bank, 512 * bank + 512)], [lq_, ls_, rq_, rs_])

    def iota(n, out, pattern, base, cm=0, whole=False):
        if whole:
            add(n, "g", lambda: g.iota(out[0], pattern, base, cm), [out], [])
        else:
            add(n, "g", lambda: g.iota(out[0], pattern, base, cm, allow_small_or_imprecise_dtypes=True), [out], [])

    def dma(n, q, sem, out, in_, outs, ins):
        add(n, q, lambda: Q[q].dma_start(out, in_), outs, ins, ("d_" + sem, 16))

    eng = topo.engines(core, hs[0])
    near = [topo.addr(h, core) for h in hs]

    def write(n, which, out, src, view, sem):
        rid, pid = near[which]
        add(n, "g", lambda: g.remote_dma(out, src, T.sem[sem], T.sem.lo, pid, rid, bits(eng)), [], [view], ("lo", len(eng)))
        left.setdefault(sem, []).append(len(ops) - 1)

    def send(n, s):
        lo = 128 * s + live(s)
        cq, cs = B("oq", lo, lo + A), B("osn", lo, lo + A)
        write(n, 0, T.rq[:, A * s:A * s + A].bitcast(dt.uint8), cq[0].bitcast(dt.uint8), cq, "ra%d" % s)
        write(n, 1, T.rs[:, A * s:A * s + A], cs[0], cs, "ra%d" % s)

    def take(n, out, tmp, k):
        ts(n, out, B(tmp, 15, k, 16), col("cd", 4), O.add)

    def wrap(mark, out, free, tmp, k):
        scan("hold" + mark, B(tmp, 0, k), B("h16", 0, k), free, 0.0, O.add, O.min)
        take("take" + mark, out, tmp, k)

    IDS = B("iot", 0, C)
    PF = B("pf", 16, 272)
    OS = B("osm", 0, 2)
    PW = B("pw", 0, 12)
    BEST = col("boff", 0)

    def xcodes(t):
        return (B("lq", 0, C), B("ls", 0, C)) if t == 0 else (B("xq%d" % t), B("xs%d" % t))

    def unpack(n, w, q, s):
        for b in range(4):
            mm(n, b, w, B("eq", 128 * b, 128 * b + 128), B("es", 128 * b, 128 * b + 128), q, s)

    def planes_of_d():
        for b in range(4):
            act("dx", plane("dx", b, C), B("ps", 512 * b, 512 * b + C))

    def along_paths(paths, queues):
        for b, q in enumerate(queues):
            move("dp", q, plane("dp", b, hi=C), ind(plane("dx", b, C), paths))

    def tables(first):
        levels = [("p1", "w1"), ("p2", "w2"), ("p4", "w4"), ("p8", "w8")]
        for lv, (p, w) in enumerate(levels):
            mark = str(lv) + ("" if first else "'")
            if lv > 0 or not first:
                wrap(mark, B(w), B(p, 0, C), "sc", C)
            if lv < 3:
                act("double" + mark, B(levels[lv + 1][0]), ind(B(p, 0, C), B(w)))
            if lv > 0:
                act("tm" + mark, B("tm"), B("ta"), IDENT, col("cf", 1 + lv))
                ts("tn" + mark, B("tn"), B("ta"), col("cd", lv), O.mult)
            m, n = ("tm", "tn") if lv else ("im", "inn")
            tt("step" + mark, B("ta") if lv < 3 else B("tw", 0, C), ind(B(m), B(w)), B(n), O.add)

    def best(t):
        mm("scores", 4, C, B("upq", 128 * t, 128 * t + 128), B("ups", 128 * t, 128 * t + 128), *xcodes(t))
        scan("eb", B("eb", 1, C), B("ps", 2048, 2048 + C - 1), B("cap", 1, C), -BIG, O.max, O.min)
        tt("npr", B("npr"), B("ps", 2048, 2048 + C), B("eb"), O.is_le)
        scan("cb", B("cb"), B("npr"), B("ge" if t else "ge0"), 0.0, O.min, O.add)
        ts("boff", BEST, col("cb", C - 1), -64.0, O.mult, col("cd", 8 if t else 5), O.add)

    def places(out):
        tt("places", B("vl", 1, 33), ind(B("cum"), OS), B("tj", 0, 32), O.is_ge)
        tt("places", B("rr", 1, 33), ind(B("cum"), OS), B("tj", 32, 64), O.add)
        scan("es", B("es1"), B("vl", 0, 32), B("rr", 1, 33), 0.0, O.mult, O.max)
        copy("ew", B(out), B("es1", 7, 32, 8))

    def new_parents(t):
        tt("qt", B("q_t"), ind(B("cum", 32), col("osm", 2)), B("tj", 96, 112), O.subtract)
        tt("qi", B("q_i"), ind(B("cum"), col("osm", 2)), B("q_t"), O.is_le)
        tt("qd", B("q_d"), B("q_i"), B("tj", 112, 128), O.mult)
        if t == 0:
            take("pwr", B("pwr", 0, 12), "pws", C)
            tt("qn", B("q_o", 0, 12), B("pwr", 0, 12), B("q_d", 0, 12), O.max)
        else:
            tt("qn", B("q_o"), ind(B("tw"), BEST), B("q_d"), O.max)
        copy("qo", B("qo"), B("q_o", 0, 12))
        act("vals", B("vals", 1, C + 1), ind(B("iot"), PW))
        act("own", B("vals", 0, C, 32), B("vals", 1, C, 32))
        copy("scatter", ind(B("p1"), B("qo")), B("vals", 0, C))

    def mirror(t):
        tt("mt", B("m_t"), B("rr", 0, 32), B("ti", 64, 96), O.subtract)
        tt("mn", B("m_n"), B("m_t"), B("tj", 64, 96), O.max)
        scan("ms", B("m_s"), B("vl", 0, 32), B("m_n"), 0.0, O.mult, O.min)
        ts("mw", B("mw"), B("m_s", 7, 32, 8), -1.0, O.mult)
        copy("mf", B("mf"), ind(PF, B("mw")))
        wrap("m", B("mo"), B("mf"), "ms", A)
        act("srf0", B("srf"), B("iot", 0, W))
        copy("srf", ind(B("srf"), B("mo")), B("iot", C, W))
        wrap("s", B("sro"), B("srf", 0, C), "srs", C)
        for b in range(4):
            copy("split", plane("xp", b, hi=C), B("xw%d" % t, b, 4 * C, 4))
            act("xm", plane("xm", b, A), ind(plane("xp", b), B("mo")))

    def make_p(t, off, queues):
        for b, q in enumerate(queues):
            move("p", q, B("ph", b, 4 * A, 4), ind(plane("dp", b), B(off, 0, 4)))
        quant("qp", B("oq", 256 * t, 256 * t + 128), B("osn", 256 * t, 256 * t + 128), B("ph", 0, 512))

    def layer(t):
        s = 2 * t
        if t == 0:
            pq, psc, at = B("oq", 0, 128), B("osn", 0, 128), 0
        else:
            lo = landing(s)
            arrival("la%d" % s, t, [0, 1], B("lq", lo, lo + A), B("ls", lo, lo + A))
            pq, psc, at = B("lq", lo - A, lo + A), B("ls", lo - A, lo + A), A
        for b in range(4):
            mm("layer", 4 + b, 128, B("wq", 128 * b, 128 * b + 128), B("wsc", 128 * b, 128 * b + 128), pq, psc)
        for b in range(4):
            lo = 512 * (4 + b) + at
            act("relu", B("ph", 512 + b, 768, 4), B("ps", lo, lo + A), ActivationFunctionType.Relu, 0.03125)
        base = 128 * (s + 1)
        quant("qh", B("oq", base, base + 128), B("osn", base, base + 128), B("ph", 256, 768))
        send("sendh", s + 1)

    def update(t):
        part[0] = t + 1
        lo = landing(2 * t + 1)
        arrival("la%d" % (2 * t + 1), t, [0, 1], B("lq", lo, lo + A), B("ls", lo, lo + A))
        unpack("back", 128, B("lq", lo - A, lo + A), B("ls", lo - A, lo + A))
        nx = "xw%d" % (t + 1)
        for b in range(4):
            tt("sum", plane("xp", b, lo=C), B("ps", 512 * b + A, 512 * b + 128), plane("xm", b, A), O.add)
        for q, b, c0, c1 in [("s", 0, 0, 12), ("s", 1, 0, 12), ("v", 2, 0, 12), ("v", 3, 0, 8), ("s", 3, 8, 12)]:
            move("gather", q, B(nx, 64 * c0 + b, 64 * c1, 4), ind(plane("xp", b), B("sro", c0, c1)))
        quant("qx", *xcodes(t + 1), B(nx))
        if t + 1 < R:
            act("upper", B("t2a"), ind(B("tw", 0, C), B("w8")))
            act("upper", B("tw", C, 2 * C), ind(B("t2a"), B("w8")))

    def rest(t):
        layer(t)
        new_parents(t)
        mirror(t)
        if t + 1 < R:
            tt("isroot", B("rootf"), B("p1", 0, C), IDS, O.is_equal)
            tables(False)
        else:
            act("opf", B("opf"), B("p1", 0, C))
            dma("op", "y", "op", T.op[:], T.opf[0:128:16, :], [], [B("opf")])
        update(t)

    dma("par", "y", "par", T.pari[:], T.par[:], [B("pari")], [])
    dma("x", "y", "x", T.xw0[:], T.x[:], [B("xw0")], [])
    dma("u", "y", "u", T.ub[:], T.u[:], [B("ub")], [])
    dma("wc", "y", "wc", T.wq[:].bitcast(dt.uint8), T.wc[:], [B("wq")], [B("xw0"), B("ub")])
    dma("ws", "y", "ws", T.wsc[:], T.ws[:], [B("wsc")], [B("xw0"), B("ub")])
    dma("v", "y", "v", T.vb[:], T.v[:], [B("vb")], [B("wq")])

    iota("pi", B("pi"), [[0, 1]], 0, 1, True)
    fill("half", B("srf"), 0.5)
    scan("iot", B("iot", 0, W), B("srf"), B("srf"), -1.0, O.add, O.add)
    iota("jm16", B("jm16"), [[0, 12], [1, 16]], 0)
    iota("kap", B("kap"), [[1, 6], [0, 32]], 0)
    iota("ti0", B("ti", 0, 32), [[-16, 4], [-32, 8]], 224)
    iota("ti0", B("ti", 32, 64), [[16, 4], [0, 8]], 0)
    iota("ti64", B("ti", 64, 96), [[0, 4], [-64, 8]], 479)
    iota("ti64", B("ti", 96, 112), [[0, 8], [-16, 2]], 32)
    iota("ti64", B("ti", 112, 128), [[16, 16]], C)
    for n, view, c in ([("tail", B("zt", 512, 520), 0), ("tw0", B("tw", 384, 392), 0), ("small", B("pf", 0, 16), -1),
                        ("small", col("vl", 0), 0), ("small", col("rr", 0), 0), ("small", B("tw", C, C + 8), 0)]
                       + [("dpz", plane("dp", b, lo=C), 0) for b in range(4)] + [("xpz", plane("xp", b, lo=C), 0) for b in range(4)]):
        iota(n, view, [[0, width(view)]], c)
    for n, view, c in [("zero", B("ph", 256, 512), 0.0), ("cum0", B("cum"), 0.0), ("eb0", col("eb", 0), -BIG),
                       ("cap", B("cap"), BIG), ("capend", B("cap", 0, C, 32), -BIG),
                       ("m1", B("m1"), 0.0), ("m1", B("m1", 0, C, 32), -1.0)]:
        lin(n, view, B("iot", 0, width(view)), 0.0, c)
    for j, (sh, m) in enumerate([(0, 15), (0, 1), (1, 1), (2, 1), (3, 1)]):
        ts("ci", col("ci", j), col("pi", 0), sh, O.logical_shift_right, m, O.bitwise_and)
    copy("cf", B("cf", 0, 5), B("ci"))
    lin("q1", col("cf", 8), col("cf", 0), 1.0, 1.0)
    for j in (6, 7):
        lin("q8", col("cf", j), col("cf", 4), -8.0, col("cf", 0))
    lin("q2", col("cd", 6), col("cf", 0), 0.5, 0.0)
    lin("q2", col("cf", 5), col("cf", 1), -0.5, col("cd", 6))
    lin("cd03", B("cd", 0, 4), B("cf", 1, 5), -1.0, 1.0)
    ts("cd4", col("cd", 4), col("cf", 0), 15.0, O.is_lt, 256.0, O.mult)
    lin("cd5", col("cd", 5), col("cf", 6), 32.0, -32.0)
    lin("cd8", col("cd", 7), col("cf", 5), 32.0, -32.0)
    lin("cd8", col("cd", 8), col("cf", 1), float(C), col("cd", 7))
    lin("negq", col("cd", 9), col("cf", 0), -1.0, 0.0)
    ts("im", B("im"), IDS, col("cf", 1), O.mult)
    ts("inn", B("inn"), IDS, col("cd", 0), O.mult)
    ts("ha", B("ha"), B("jm16"), col("cf", 0), O.is_le, 1024.0, O.mult)
    ts("hb", B("hb"), B("jm16"), col("cf", 8), O.is_equal, -256.0, O.mult)
    tt("h16", B("h16"), B("ha"), B("hb"), O.add)
    ts("osm", B("osm", 0, 2), B("cf", 6, 8), -32.0, O.mult, 224.0, O.add)
    ts("osm", col("osm", 2), col("cf", 5), 6.0, O.min, 32.0, O.mult)
    lin("tj0", B("tj", 0, 32), B("ti", 0, 32), 1.0, col("cd", 9))
    lin("tj32", B("tj", 32, 64), B("ti", 32, 64), 1.0, col("cf", 0))
    lin("tj64", B("tj", 64, 96), B("tj", 0, 32), -1.0, -63.0)
    lin("tj96", B("tj", 96, 112), B("ti", 96, 112), 1.0, col("cd", 9))
    lin("tj112", B("tj", 112, 128), B("ti", 112, 128), 1.0, col("cf", 0))
    act("sent", B("pf", 16 + C, 272), B("iot", C, W))
    for lo in (0, 256):
        out, zero = B("zt", lo, lo + 256), B("ph", 256, 512)
        add("unit%d" % (lo // 256), "g",
            lambda out=out, zero=zero, lo=lo: g.affine_select(out[0], zero[0], [[1, 256]], O.not_equal, 1.0, lo - 3, -4), [out], [zero])
    for b in range(4):
        quant("eq%d" % b, B("eq", 128 * b, 128 * b + 128), B("es", 128 * b, 128 * b + 128), B("zt", 3 - b, 515 - b))
    quant("qu", B("uq"), B("us"), B("ub"))
    for t in range(R):
        part[0] = t // 2
        off = B("oc16", 8 * t, 8 * t + 8)
        ts("oc%d" % t, off, B("iot", 0, 128, 16), float(t), O.add)
        copy("pick%d" % t, w32(B("upq", 128 * t, 128 * t + 128)), ind(w32(B("uq")), off))
        act("picks%d" % t, B("ups", 128 * t, 128 * t + 128), ind(B("us"), off))
    for t, n, j in [(0, "0", 6), (1, "", 5)]:
        part[0] = t
        ts("ge" + n, B("ge" + n), B("kap"), col("cf", j), O.is_equal, 1.0 / 64, O.mult)
        ts("gend" + n, B("ge" + n, 31, C, 32), B("kap", 31, C, 32), col("cf", j), O.is_equal, -63.0 / 64, O.mult)
    part[0] = 2
    quant("qv", B("vq"), B("vs"), B("vb"))
    part[0] = 0

    quant("qx", B("lq", 0, C), B("ls", 0, C), B("xw0"))
    write("sendx", 0, T.gq[:].bitcast(dt.uint8), T.lq[:, 0:C].bitcast(dt.uint8), B("lq", 0, C), "ra0")
    write("sendx", 1, T.gs[:], T.ls[:, 0:C], B("ls", 0, C), "ra0")
    copy("w1", B("w1"), B("pari"))
    act("p1", B("p1", 0, C), ind(IDS, B("w1")))
    tables(True)
    act("p16", B("iot", W, W + C), ind(B("p8"), B("w8")))
    best(0)
    copy("pw", B("pw", 0, 32, 2), ind(B("tw", 0, C + 8), BEST))
    ts("pw", B("pw", 1, 32, 2), ind(B("tw", 0, C + 8), BEST), float(W), O.add)
    copy("pf", B("pf", 16, 16 + C // 2), ind(B("iot"), B("pw", 0, 6)))
    act("pf", B("pf", 16 + C // 2, 16 + C), ind(B("iot"), B("pw", 6, 12)))
    wrap("p", B("pwu", 0, 12), B("pf", 16, 16 + C), "pws", C)
    write("sendp", 1, T.gp[:], T.pwu[:], B("pwu"), "rap")
    tt("fl", B("fl"), B("pf", 16, 16 + C), B("pf", 15, 15 + C), O.is_equal)
    scan("cum", B("cum", 1, C + 1), B("fl"), B("ph", 256, 256 + C), 0.0, O.add, O.add)
    places("ew0")
    write("sende", 1, T.gl[:], T.ew0[:], B("ew0"), "ral")
    arrival("la0", 0, [0, 1], B("fq"), B("fs"))
    unpack("unpack", C, B("fq"), B("fs"))
    planes_of_d()
    arrival("lap", 0, [1], B("fp"))
    along_paths(B("fp", 0, 12), "svsv")
    arrival("lal", 0, [1], B("fo"))
    make_p(0, "fo", "vsvs")
    rest(0)

    for t in range(1, R):
        best(t)
        unpack("unpack", C, *xcodes(t))
        copy("pw", B("pw", 0, 16), ind(B("tw"), BEST))
        planes_of_d()
        along_paths(PW, "ssss")
        copy("fl", B("fl"), ind(B("rootf"), PW))
        scan("cum", B("cum", 1, C + 1), B("fl"), B("m1"), 0.0, O.add, O.add)
        places("ew")
        make_p(t, "ew", "vvss")
        send("send", 2 * t)
        act("pf", B("pf", 16, 16 + C), ind(IDS, PW))
        rest(t)

    xq, xs = xcodes(R)
    mm("y", 4, C, B("vq"), B("vs"), xq, xs)
    dma("oc", "y", "oc", T.oc[:], xq[0].bitcast(dt.uint8), [], [xq])
    for k in range(4):
        dma("scales", "s" if k % 2 else "y", "s%d" % k, T.osc[4 * k:4 * k + 4, :], T.xs3[32 * k:32 * k + 4, :], [], [xs])
    copy("y", B("yf"), B("ps", 2048, 2048 + C))
    dma("y", "s", "y", T.y[:], T.yf[:], [], [B("yf")])

    named, lines = {}, {None: [i for i, o in enumerate(ops) if o[0] is None]}
    for i, o in enumerate(ops):
        named.setdefault((o[0],) + o[5], []).append(i)
    for q in Q:
        lines[q] = [i for k, names in enumerate([FIRST, ROUND, ROUND, LAST]) for n in names[q].split() for i in named.get((q, k, n), [])]
    order, out = [], set()
    while len(order) < len(ops):
        heads = [line for line in lines.values() if line and all(d in out for d in ops[line[0]][2] + ops[line[0]][6])]
        assert heads
        for line in heads:
            order.append(line.pop(0))
            out.add(order[-1])
    for o in ops:
        for d in o[2]:
            ops[d][4] = True
    token, total, waited = {}, {}, {}
    for i in order:
        o = ops[i]
        name, k = o[3] if o[3] else (CNT[o[0]], 1 if o[4] else 0)
        total[name] = total.get(name, 0) + k
        token[i] = (name, total[name])
    for i in order:
        q, call, deps, sem, needed = ops[i][:5]
        if q is None:
            continue
        want = {}
        for d in deps:
            name, v = token[d]
            want[name] = max(want.get(name, 0), v)
        for name in sorted(want):
            if waited.get((q, name), 0) < want[name]:
                Q[q].wait_ge(T.sem[name], want[name])
                waited[(q, name)] = want[name]
        ins = call()
        if sem is None:
            if needed:
                ins.then_inc(T.sem[CNT[q]], 1)
        elif sem[0] != "lo":
            ins.then_inc(T.sem[sem[0]], sem[1])
    for name in sorted(total):
        if total[name] and max([waited.get((q, name), 0) for q in Q]) < total[name]:
            g.wait_ge(T.sem[name], total[name])
